import numpy as np
import ml_dtypes


def mxq(x, axis, fmt="e4m3"):
    dtype, down = {"e4m3": (ml_dtypes.float8_e4m3fn, 7), "e5m2": (ml_dtypes.float8_e5m2, 14)}[fmt]
    v = np.moveaxis(np.asarray(x, np.float32).astype(ml_dtypes.bfloat16).astype(np.float64), axis, -1)
    blocks = v.reshape(v.shape[:-1] + (-1, 32))
    amax = np.abs(blocks).max(-1, keepdims=True)
    byte = np.maximum(np.where(amax > 0, np.frexp(amax)[1] - 1 + 127, 0) - down, 1)
    scale = np.exp2(byte - 127.0)
    codes = (blocks / scale).astype(np.float32).astype(dtype).astype(np.float64)
    return np.moveaxis((codes * scale).reshape(v.shape), -1, axis)


WIDE = False


def mx_kscale(k):
    if not WIDE:
        return np.ones(k)
    levels = np.array([10, -10, 5, -5, 0])
    if k % 512:
        return np.exp2(np.random.permutation(np.resize(levels, k // 32))).repeat(32)
    a = np.empty((k // 512, 16))
    for p in range(k // 512):
        a[p, :8] = np.random.permutation(np.resize(levels, 8))
        for g in range(8):
            far = levels[np.abs(levels - a[p, g]) >= 10]
            a[p, g + 8] = far[np.random.randint(len(far))]
    return np.exp2(a.ravel()).repeat(32)


def f64(x):
    return np.asarray(x).astype(np.float64)


E2M1 = np.array([0.0, 0.5, 1.0, 1.5, 2.0, 3.0, 4.0, 6.0, -0.0, -0.5, -1.0, -1.5, -2.0, -3.0, -4.0, -6.0])


def pack_weight(w, fmt):
    k, n = w.shape
    w = f64(np.asarray(w, np.float32).astype(ml_dtypes.bfloat16)).reshape(k // 32, 32, n)
    amax = np.abs(w).max(1)
    if fmt == "e4m3":
        byte = np.frexp(amax)[1] - 1 + 127 - 7
    else:
        mant, ex = np.frexp(amax / 6.0)
        byte = np.where(mant > 0.5, ex, ex - 1) + 127
    byte = np.clip(np.where(amax > 0, byte, 1), 1, 254)
    scaled = (w * np.exp2(127.0 - byte)[:, None, :]).reshape(k, n).astype(np.float32)
    by_word = np.ascontiguousarray(scaled.reshape(k // 512, 128, 4, n).transpose(0, 1, 3, 2))
    if fmt == "e4m3":
        words = by_word.astype(ml_dtypes.float8_e4m3fn).view(np.uint8)
    else:
        c = by_word.astype(ml_dtypes.float4_e2m1fn).view(np.uint8) & 0xF
        words = (c[..., 0::2] | (c[..., 1::2] << 4)).reshape(k // 512, 128, 2 * n)
    return np.ascontiguousarray(words), np.ascontiguousarray(byte.astype(np.uint8).reshape(k // 512, 16, n))


def unpack_weight(words, scales, fmt):
    g, _, n = scales.shape
    words = np.ascontiguousarray(words).reshape(g, 128, n, -1)
    if fmt == "e4m3":
        vals = words.view(ml_dtypes.float8_e4m3fn).astype(np.float64)
    else:
        nib = np.empty((g, 128, n, 4), np.uint8)
        nib[..., 0::2] = words & 0xF
        nib[..., 1::2] = words >> 4
        vals = E2M1[nib]
    vals = vals * np.repeat(np.exp2(scales.astype(np.float64) - 127.0), 8, axis=1)[..., None]
    return vals.transpose(0, 1, 3, 2).reshape(g * 512, n)


O, K, R, M, T = 1024, 2560, 512, 2048, 512


def setup_inputs():
    n = np.random.standard_normal
    s = mx_kscale(K)[:, None]
    u = mx_kscale(R)[:, None]
    x = n((K, T)); x[:O] *= 6.0
    w = n((K, M)) / np.sqrt(K) / s; w[:O] /= 2.0
    p_w8 = pack_weight(w[:O], "e4m3")
    p_w4 = pack_weight(w[O:], "e2m1")
    p_up = pack_weight(n((R, M)) / np.sqrt(R) / u, "e2m1")
    return {
        "x": (x * s).astype(np.float32),
        "w8_words": p_w8[0],
        "w8_scales": p_w8[1],
        "w4_words": p_w4[0],
        "w4_scales": p_w4[1],
        "down": (0.3 * n((K, R)) / np.sqrt(K) / s * u.T).astype(np.float32),
        "up_words": p_up[0],
        "up_scales": p_up[1],
        "b": (0.3 * n(2048)).astype(np.float32),
    }


def reference(x, w8_words, w8_scales, w4_words, w4_scales, down, up_words, up_scales, b):
    x_ = mxq(f64(x), 0, "e4m3")
    w8_ = unpack_weight(w8_words, w8_scales, "e4m3")
    w4_ = unpack_weight(w4_words, w4_scales, "e2m1")
    down_ = mxq(f64(down), 0, "e4m3")
    up_ = unpack_weight(up_words, up_scales, "e2m1")
    h_ = mxq(down_.T @ x_, 0, "e4m3")
    y = w8_.T @ x_[:O] + w4_.T @ x_[O:] + up_.T @ h_
    return y + f64(b)[:, None]

@@ -1,0 +1,289 @@
+from contextlib import ExitStack
+
+import concourse.mybir as mybir
+from concourse.masks import make_identity
+
+O, K, R, M, T = 1024, 2560, 512, 2048, 512
+FLOPS = 2 * K * R * T + 2 * (K + R) * M * T
+
+F32 = mybir.dt.float32
+BF16 = mybir.dt.bfloat16
+I32 = mybir.dt.int32
+U32 = mybir.dt.uint32
+U8 = mybir.dt.uint8
+E4M3 = mybir.dt.float8_e4m3fn_x4
+E2M1 = mybir.dt.float4_e2m1fn_x4
+IDENT = mybir.ActivationFunctionType.Identity
+
+P = 128
+PACK = 4
+KP = 512
+NK = K // KP
+NO = O // KP
+NT = M // P
+SECTIONS = ((0, 512), (512, 1024), (1024, 2048))
+XV = 256
+
+
+def tile_mix_three_fm_bias_kernel(
+    tc, x, w8_words, w8_scales, w4_words, w4_scales, down, up_words, up_scales, b, out
+):
+    nc = tc.nc
+    with ExitStack() as ctx:
+        keep = ctx.enter_context(tc.tile_pool(name="keep", bufs=1))
+        group = ctx.enter_context(tc.tile_pool(name="group", bufs=2))
+        res = ctx.enter_context(tc.tile_pool(name="res", bufs=4))
+        psum = ctx.enter_context(tc.psum_pool(name="psum", bufs=1))
+        ctx.enter_context(tc.manual_schedule())
+
+        x_raw = [keep.tile([P, PACK, T], F32, name=f"x_raw{g}") for g in range(NK)]
+        d_raw = [keep.tile([P, PACK, R], F32, name=f"d_raw{g}") for g in range(NK)]
+        x_codes = [keep.tile([P, T], U32, name=f"x_codes{g}", align_bytes=64) for g in range(NK)]
+        x_scale = [keep.tile([P, T], U8, name=f"x_scale{g}", align_bytes=64) for g in range(NK)]
+        d_codes = [keep.tile([P, R], U32, name=f"d_codes{g}", align_bytes=64) for g in range(NK)]
+        d_scale = [keep.tile([P, R], U8, name=f"d_scale{g}", align_bytes=64) for g in range(NK)]
+        w8 = [keep.tile([P, NO, c1 - c0], U32, name=f"w8_{c0}", align_bytes=64) for c0, c1 in SECTIONS]
+        w4 = [keep.tile([P, NK - NO, 2 * (c1 - c0)], U8, name=f"w4_{c0}", align_bytes=64) for c0, c1 in SECTIONS]
+        w8s = keep.tile([P, M], U8, name="w8s", align_bytes=64)
+        w4s = [keep.tile([P, NK - NO, c1 - c0], U8, name=f"w4s_{c0}", align_bytes=64) for c0, c1 in ((0, 512), (512, 2048))]
+        up = keep.tile([P, 2 * M], U8, name="up", align_bytes=64)
+        ups = keep.tile([P, M], U8, name="ups", align_bytes=64)
+        b_rows = keep.tile([P, P], F32, name="b_rows")
+        ident = keep.tile([P, P], F32, name="ident")
+        b_col = keep.tile([P, NT], F32, name="b_col")
+        warm = keep.tile([P, 1], F32, name="warm")
+        h_rows = keep.tile([P, PACK, T], BF16, name="h_rows", align_bytes=64)
+        h_grp = keep.tile([P, T, PACK], BF16, name="h_grp", align_bytes=64)
+        h_codes = keep.tile([P, T], U32, name="h_codes", align_bytes=64)
+        h_scale = keep.tile([P, T], U8, name="h_scale", align_bytes=64)
+
+        nc.vector.memset(warm[:], 0.0)
+        for t in (w8s, w4s[0]):
+            flat = t[:] if len(t.shape) == 2 else t[:].rearrange("p a n -> p (a n)")
+            nc.vector.memset(flat.bitcast(I32), 0)
+        nc.gpsimd.memset(b_rows[:], 0.0)
+        make_identity(nc, ident[:])
+        nc.scalar.activation(out=warm[:], in_=warm[:], func=IDENT)
+        nc.scalar.dma_start(out=b_rows[0:NT, :], in_=b.rearrange("(g p) -> g p", p=P))
+        for t in (w4s[1], ups):
+            flat = t[:] if len(t.shape) == 2 else t[:].rearrange("p a n -> p (a n)")
+            nc.vector.memset(flat.bitcast(I32), 0)
+
+        w8_view = w8_words.rearrange("a p n i -> p a (n i)")
+        w4_view = w4_words.rearrange("a p n -> p a n")
+        w4s_view = w4_scales.rearrange("a q n -> q a n")
+
+        def load_x(g):
+            nc.sync.dma_start(
+                out=x_raw[g][:].rearrange("p j t -> p (j t)"),
+                in_=x[KP * g : KP * (g + 1), :].rearrange("(p j) t -> p (j t)", j=PACK),
+            )
+
+        def load_d(g):
+            nc.sync.dma_start(
+                out=d_raw[g][:].rearrange("p j r -> p (j r)"),
+                in_=down[KP * g : KP * (g + 1), :].rearrange("(p j) r -> p (j r)", j=PACK),
+            )
+
+        def load_w8(s):
+            c0, c1 = SECTIONS[s]
+            nc.sync.dma_start(out=w8[s][:].bitcast(I32), in_=w8_view[:, :, 4 * c0 : 4 * c1].bitcast(I32))
+
+        def load_w4(s):
+            c0, c1 = SECTIONS[s]
+            nc.sync.dma_start(out=w4[s][:].bitcast(I32), in_=w4_view[:, :, 2 * c0 : 2 * c1].bitcast(I32))
+
+        def load_w8s(eng):
+            for q in range(4):
+                eng.dma_start(
+                    out=w8s[32 * q + 4 : 32 * q + 12, :].bitcast(I32),
+                    in_=w8_scales[:, 4 * q : 4 * q + 4, :].bitcast(I32),
+                )
+
+        def load_w4s(eng, s, quads=(0, 1, 2, 3)):
+            c0, c1 = ((0, 512), (512, 2048))[s]
+            for q in quads:
+                eng.dma_start(
+                    out=w4s[s][32 * q : 32 * q + 4, :, :].bitcast(I32),
+                    in_=w4s_view[4 * q : 4 * q + 4, :, c0:c1].bitcast(I32),
+                )
+
+        def load_ups(eng):
+            for q in range(4):
+                eng.dma_start(
+                    out=ups[32 * q : 32 * q + 4, :].bitcast(I32),
+                    in_=up_scales[0, 4 * q : 4 * q + 4, :].bitcast(I32),
+                )
+
+        load_w8s(nc.gpsimd)
+        load_x(0)
+        load_d(0)
+        for g in (1, 2):
+            load_x(g)
+            load_w4s(nc.sync, 0, (2 * g - 2, 2 * g - 1))
+            load_d(g)
+        load_w8(0)
+        load_w4(0)
+        load_x(3)
+        load_x(4)
+        load_d(3)
+        load_d(4)
+        load_w8(1)
+        load_w4s(nc.sync, 1)
+        load_w4(1)
+        nc.sync.dma_start(out=up[:].bitcast(I32), in_=up_words[0].bitcast(I32))
+        load_ups(nc.sync)
+        load_w8(2)
+        load_w4(2)
+
+        def quant_x(g):
+            grp = group.tile([P, T, PACK], BF16, name="x_grp", align_bytes=64)
+            for copy, c0, c1 in ((nc.vector.tensor_copy, 0, XV), (nc.scalar.copy, XV, T)):
+                copy(
+                    out=grp[:, c0:c1, :].rearrange("p (c i) j -> p c j i", i=4),
+                    in_=x_raw[g][:, :, c0:c1].rearrange("p j (c i) -> p c j i", i=4),
+                )
+            nc.vector.quantize_mx(
+                out=x_codes[g][:].bitcast(E4M3), scales=x_scale[g][:], in_=grp[:].rearrange("p t j -> p (t j)")
+            )
+
+        def spread_d(g, grp, m0, m1):
+            for copy, j0, j1 in ((nc.vector.tensor_copy, 0, 2), (nc.scalar.copy, 2, 4)):
+                copy(
+                    out=grp[:, j0:j1, m0:m1, :].rearrange("p t m j -> p m j t"),
+                    in_=d_raw[g][:].rearrange("p j (m t) -> p m j t", t=4)[:, m0:m1, :, j0:j1],
+                )
+
+        def quant_d(g, grp, j0, j1):
+            nc.vector.quantize_mx(
+                out=d_codes[g][:, P * j0 : P * j1].bitcast(E4M3),
+                scales=d_scale[g][:, P * j0 : P * j1],
+                in_=grp[:, j0:j1, :, :].rearrange("p t m j -> p (t m j)"),
+            )
+
+        def h_pass(g, j):
+            nc.tensor.matmul_mx(
+                out=h_acc[j][:],
+                lhsT=d_codes[g][:, P * j : P * (j + 1)].bitcast(E4M3),
+                lhsT_scale=d_scale[g][:, P * j : P * (j + 1)],
+                rhs=x_codes[g][:].bitcast(E4M3),
+                rhs_scale=x_scale[g][:],
+                start=(g == 0),
+                stop=(g == NK - 1),
+            )
+
+        def where(n):
+            c = P * n
+            s = 0 if c < 512 else (1 if c < 1024 else 2)
+            return s, c - SECTIONS[s][0]
+
+        def y_pass(n, g, t0=0, t1=T):
+            s, c = where(n)
+            ss, cc = (0, P * n) if s == 0 else (1, P * n - 512)
+            if g < NO:
+                lhsT = w8[s][:, g, c : c + P].bitcast(E4M3)
+                lscale = w8s[4 + 4 * g : P, P * n : P * (n + 1)]
+            else:
+                lhsT = w4[s][:, g - NO, 2 * c : 2 * (c + P)].bitcast(E2M1)
+                lscale = w4s[ss][:, g - NO, cc : cc + P]
+            nc.tensor.matmul_mx(
+                out=y_acc[n][:], lhsT=lhsT, lhsT_scale=lscale,
+                rhs=x_codes[g][:, t0:t1].bitcast(E4M3), rhs_scale=x_scale[g][:, t0:t1],
+                start=(g == 0), stop=False,
+            )
+
+        def up_pass(n, t0=0, t1=T):
+            nc.tensor.matmul_mx(
+                out=y_acc[n][:],
+                lhsT=up[:, 2 * P * n : 2 * P * (n + 1)].bitcast(E2M1), lhsT_scale=ups[:, P * n : P * (n + 1)],
+                rhs=h_codes[:, t0:t1].bitcast(E4M3), rhs_scale=h_scale[:, t0:t1],
+                start=False, stop=True,
+            )
+
+        def finish(n):
+            o = res.tile([P, T], F32, name="o")
+            if n % 2 == 0:
+                nc.scalar.activation(out=o[:], in_=y_acc[n][:], func=IDENT, bias=b_col[:, n : n + 1])
+            else:
+                nc.vector.tensor_scalar_add(o[:], y_acc[n][:], b_col[:, n : n + 1])
+            nc.sync.dma_start(out=out[P * n : P * (n + 1), :], in_=o[:])
+
+        y_acc = {}
+
+        def open_bank(n):
+            y_acc[n] = psum.tile([P, T], F32, name=f"bank{n % 8}")
+
+        b_turn = psum.tile([P, P], F32, name="bank0")
+        nc.tensor.transpose(b_turn[:], b_rows[:], ident[:])
+        h_acc = [psum.tile([P, T], F32, name=f"bank{4 + j}") for j in range(PACK)]
+        for g in range(3):
+            quant_x(g)
+            if g == 0:
+                nc.scalar.copy(out=b_col[:], in_=b_turn[:, 0:NT])
+            d_grp = group.tile([P, PACK, P, PACK], BF16, name="d_grp", align_bytes=64)
+            spread_d(g, d_grp, 0, P)
+            quant_d(g, d_grp, 0, 4)
+            for j in range(PACK):
+                h_pass(g, j)
+        for n in range(4):
+            open_bank(n)
+        for g in range(3):
+            for n in range(4):
+                y_pass(n, g)
+        quant_x(3)
+        for n in range(4):
+            y_pass(n, 3)
+        quant_x(4)
+        for n in range(4):
+            y_pass(n, 4)
+        d_grp = group.tile([P, PACK, P, PACK], BF16, name="d_grp", align_bytes=64)
+        spread_d(3, d_grp, 0, P)
+        quant_d(3, d_grp, 0, 4)
+        for j in range(PACK):
+            h_pass(3, j)
+        d_grp = group.tile([P, PACK, P, PACK], BF16, name="d_grp", align_bytes=64)
+        spread_d(4, d_grp, 0, P)
+        for j in range(PACK):
+            quant_d(4, d_grp, j, j + 1)
+        for j in range(PACK):
+            h_pass(4, j)
+        for j in range(PACK):
+            copy = nc.scalar.copy if j % 2 == 0 else nc.vector.tensor_copy
+            copy(out=h_rows[:, j, :], in_=h_acc[j][:])
+        for n in range(4, 8):
+            open_bank(n)
+        for g in range(NO):
+            for n in range(4, 8):
+                y_pass(n, g)
+        for copy, c0, c1 in ((nc.vector.tensor_copy, 0, 320), (nc.scalar.copy, 320, T)):
+            copy(out=h_grp[:, c0:c1, :], in_=h_rows[:, :, c0:c1].rearrange("p j t -> p t j"))
+        nc.vector.quantize_mx(
+            out=h_codes[:].bitcast(E4M3), scales=h_scale[:], in_=h_grp[:].rearrange("p t j -> p (t j)")
+        )
+        for n in range(4, 8):
+            for g in range(NO, NK):
+                y_pass(n, g)
+        for n in range(8):
+            up_pass(n)
+            finish(n)
+        for n in range(8, NT - 1):
+            open_bank(n)
+            for g in range(NK):
+                y_pass(n, g)
+            up_pass(n)
+            finish(n)
+        n = NT - 1
+        o = res.tile([P, T], F32, name="o")
+        for q in range(4):
+            y_acc[n] = psum.tile([P, P], F32, name=f"bank{q}")
+            for g in range(NK):
+                y_pass(n, g, P * q, P * (q + 1))
+            up_pass(n, P * q, P * (q + 1))
+            t0, t1 = P * q, P * (q + 1)
+            if q % 2 == 1:
+                nc.scalar.activation(out=o[:, t0:t1], in_=y_acc[n][:], func=IDENT, bias=b_col[:, n : n + 1])
+            else:
+                nc.vector.tensor_scalar_add(o[:, t0:t1], y_acc[n][:], b_col[:, n : n + 1])
+            if q > 0:
+                s0 = 0 if q == 1 else t0
+                nc.sync.dma_start(out=out[P * n : P * (n + 1), s0:t1], in_=o[:, s0:t1])

@@ -21,8 +21,11 @@ KP = 512
 NK = K // KP
 NO = O // KP
 NT = M // P
-SECTIONS = ((0, 512), (512, 1024), (1024, 2048))
+BANKS = 8
+EARLY = 12
+SECTIONS = ((0, BANKS), (BANKS, EARLY), (EARLY, NT))
 XV = 256
+GAP_PASSES = 8
 
 
 def tile_mix_three_fm_bias_kernel(
@@ -32,7 +35,6 @@ def tile_mix_three_fm_bias_kernel(
     with ExitStack() as ctx:
         keep = ctx.enter_context(tc.tile_pool(name="keep", bufs=1))
         group = ctx.enter_context(tc.tile_pool(name="group", bufs=2))
-        res = ctx.enter_context(tc.tile_pool(name="res", bufs=4))
         psum = ctx.enter_context(tc.psum_pool(name="psum", bufs=1))
         ctx.enter_context(tc.manual_schedule())
 
@@ -42,36 +44,29 @@ def tile_mix_three_fm_bias_kernel(
         x_scale = [keep.tile([P, T], U8, name=f"x_scale{g}", align_bytes=64) for g in range(NK)]
         d_codes = [keep.tile([P, R], U32, name=f"d_codes{g}", align_bytes=64) for g in range(NK)]
         d_scale = [keep.tile([P, R], U8, name=f"d_scale{g}", align_bytes=64) for g in range(NK)]
-        w8 = [keep.tile([P, NO, c1 - c0], U32, name=f"w8_{c0}", align_bytes=64) for c0, c1 in SECTIONS]
-        w4 = [keep.tile([P, NK - NO, 2 * (c1 - c0)], U8, name=f"w4_{c0}", align_bytes=64) for c0, c1 in SECTIONS]
-        w8s = keep.tile([P, M], U8, name="w8s", align_bytes=64)
-        w4s = [keep.tile([P, NK - NO, c1 - c0], U8, name=f"w4s_{c0}", align_bytes=64) for c0, c1 in ((0, 512), (512, 2048))]
+        w8 = [keep.tile([P, NO, P * (n1 - n0)], U32, name=f"w8_{n0}", align_bytes=64) for n0, n1 in SECTIONS]
+        w4 = [keep.tile([P, NK - NO, 2 * P * (n1 - n0)], U8, name=f"w4_{n0}", align_bytes=64) for n0, n1 in SECTIONS]
+        w8s = keep.tile([P, NO, M], U8, name="w8s", align_bytes=64)
+        w4s = keep.tile([P, NK - NO, M], U8, name="w4s", align_bytes=64)
         up = keep.tile([P, 2 * M], U8, name="up", align_bytes=64)
         ups = keep.tile([P, M], U8, name="ups", align_bytes=64)
         b_rows = keep.tile([P, P], F32, name="b_rows")
         ident = keep.tile([P, P], F32, name="ident")
         b_col = keep.tile([P, NT], F32, name="b_col")
-        warm = keep.tile([P, 1], F32, name="warm")
         h_rows = keep.tile([P, PACK, T], BF16, name="h_rows", align_bytes=64)
         h_grp = keep.tile([P, T, PACK], BF16, name="h_grp", align_bytes=64)
         h_codes = keep.tile([P, T], U32, name="h_codes", align_bytes=64)
         h_scale = keep.tile([P, T], U8, name="h_scale", align_bytes=64)
+        res = [keep.tile([P, T], F32, name=f"res{n}") for n in range(NT)]
 
-        nc.vector.memset(warm[:], 0.0)
-        for t in (w8s, w4s[0]):
-            flat = t[:] if len(t.shape) == 2 else t[:].rearrange("p a n -> p (a n)")
-            nc.vector.memset(flat.bitcast(I32), 0)
         nc.gpsimd.memset(b_rows[:], 0.0)
+        nc.vector.memset(w8s[:].rearrange("p a n -> p (a n)").bitcast(I32), 0)
+        nc.vector.memset(w4s[:].rearrange("p a n -> p (a n)").bitcast(I32), 0)
+        nc.vector.memset(ups[:].bitcast(I32), 0)
         make_identity(nc, ident[:])
-        nc.scalar.activation(out=warm[:], in_=warm[:], func=IDENT)
-        nc.scalar.dma_start(out=b_rows[0:NT, :], in_=b.rearrange("(g p) -> g p", p=P))
-        for t in (w4s[1], ups):
-            flat = t[:] if len(t.shape) == 2 else t[:].rearrange("p a n -> p (a n)")
-            nc.vector.memset(flat.bitcast(I32), 0)
 
         w8_view = w8_words.rearrange("a p n i -> p a (n i)")
         w4_view = w4_words.rearrange("a p n -> p a n")
-        w4s_view = w4_scales.rearrange("a q n -> q a n")
 
         def load_x(g):
             nc.sync.dma_start(
@@ -85,56 +80,45 @@ def tile_mix_three_fm_bias_kernel(
                 in_=down[KP * g : KP * (g + 1), :].rearrange("(p j) r -> p (j r)", j=PACK),
             )
 
-        def load_w8(s):
-            c0, c1 = SECTIONS[s]
-            nc.sync.dma_start(out=w8[s][:].bitcast(I32), in_=w8_view[:, :, 4 * c0 : 4 * c1].bitcast(I32))
+        def load_w8(s, g0=0, g1=NO):
+            n0, n1 = SECTIONS[s]
+            nc.sync.dma_start(
+                out=w8[s][:, g0:g1, :].bitcast(I32), in_=w8_view[:, g0:g1, 4 * P * n0 : 4 * P * n1].bitcast(I32)
+            )
 
-        def load_w4(s):
-            c0, c1 = SECTIONS[s]
-            nc.sync.dma_start(out=w4[s][:].bitcast(I32), in_=w4_view[:, :, 2 * c0 : 2 * c1].bitcast(I32))
+        def load_w4(s, g0=NO, g1=NK):
+            n0, n1 = SECTIONS[s]
+            nc.sync.dma_start(
+                out=w4[s][:, g0 - NO : g1 - NO, :].bitcast(I32),
+                in_=w4_view[:, g0 - NO : g1 - NO, 2 * P * n0 : 2 * P * n1].bitcast(I32),
+            )
 
-        def load_w8s(eng):
-            for q in range(4):
-                eng.dma_start(
-                    out=w8s[32 * q + 4 : 32 * q + 12, :].bitcast(I32),
-                    in_=w8_scales[:, 4 * q : 4 * q + 4, :].bitcast(I32),
-                )
+        def load_scales(eng, plane, scales, first):
+            rows = scales.rearrange("a q n -> q a n")
+            for r in range(4):
+                eng.dma_start(out=plane[first + r : P : 32].bitcast(I32), in_=rows[r:16:4].bitcast(I32))
 
-        def load_w4s(eng, s, quads=(0, 1, 2, 3)):
-            c0, c1 = ((0, 512), (512, 2048))[s]
-            for q in quads:
-                eng.dma_start(
-                    out=w4s[s][32 * q : 32 * q + 4, :, :].bitcast(I32),
-                    in_=w4s_view[4 * q : 4 * q + 4, :, c0:c1].bitcast(I32),
-                )
-
-        def load_ups(eng):
-            for q in range(4):
-                eng.dma_start(
-                    out=ups[32 * q : 32 * q + 4, :].bitcast(I32),
-                    in_=up_scales[0, 4 * q : 4 * q + 4, :].bitcast(I32),
-                )
-
-        load_w8s(nc.gpsimd)
         load_x(0)
-        load_d(0)
-        for g in (1, 2):
+        nc.sync.dma_start(out=b_rows[0:NT, :], in_=b.rearrange("(g p) -> g p", p=P))
+        load_scales(nc.sync, w8s, w8_scales, 4)
+        load_w8(0, 0, 1)
+        load_x(1)
+        load_w8(0, 1, 2)
+        load_x(2)
+        load_scales(nc.sync, w4s, w4_scales, 0)
+        load_w4(0, 2, 3)
+        for g in (3, 4):
             load_x(g)
-            load_w4s(nc.sync, 0, (2 * g - 2, 2 * g - 1))
-            load_d(g)
-        load_w8(0)
-        load_w4(0)
-        load_x(3)
-        load_x(4)
-        load_d(3)
-        load_d(4)
+            load_w4(0, g, g + 1)
         load_w8(1)
-        load_w4s(nc.sync, 1)
         load_w4(1)
-        nc.sync.dma_start(out=up[:].bitcast(I32), in_=up_words[0].bitcast(I32))
-        load_ups(nc.sync)
+        for g in range(NK):
+            load_d(g)
         load_w8(2)
         load_w4(2)
+        nc.sync.dma_start(out=up[:].bitcast(I32), in_=up_words[0].bitcast(I32))
+        for r in range(4):
+            nc.sync.dma_start(out=ups[r:P:32, :].bitcast(I32), in_=up_scales[0, r:16:4, :].bitcast(I32))
 
         def quant_x(g):
             grp = group.tile([P, T, PACK], BF16, name="x_grp", align_bytes=64)
@@ -147,19 +131,24 @@ def tile_mix_three_fm_bias_kernel(
                 out=x_codes[g][:].bitcast(E4M3), scales=x_scale[g][:], in_=grp[:].rearrange("p t j -> p (t j)")
             )
 
-        def spread_d(g, grp, m0, m1):
+        def spread_d(g):
+            grp = group.tile([P, PACK, P, PACK], BF16, name="d_grp", align_bytes=64)
             for copy, j0, j1 in ((nc.vector.tensor_copy, 0, 2), (nc.scalar.copy, 2, 4)):
                 copy(
-                    out=grp[:, j0:j1, m0:m1, :].rearrange("p t m j -> p m j t"),
-                    in_=d_raw[g][:].rearrange("p j (m t) -> p m j t", t=4)[:, m0:m1, :, j0:j1],
+                    out=grp[:, j0:j1, :, :].rearrange("p t m j -> p m j t"),
+                    in_=d_raw[g][:].rearrange("p j (m t) -> p m j t", t=4)[:, :, :, j0:j1],
                 )
+            return grp
 
-        def quant_d(g, grp, j0, j1):
-            nc.vector.quantize_mx(
-                out=d_codes[g][:, P * j0 : P * j1].bitcast(E4M3),
-                scales=d_scale[g][:, P * j0 : P * j1],
-                in_=grp[:, j0:j1, :, :].rearrange("p t m j -> p (t m j)"),
-            )
+        def quant_d(g, grp, parts):
+            width = PACK // parts
+            for j0 in range(0, PACK, width):
+                j1 = j0 + width
+                nc.vector.quantize_mx(
+                    out=d_codes[g][:, P * j0 : P * j1].bitcast(E4M3),
+                    scales=d_scale[g][:, P * j0 : P * j1],
+                    in_=grp[:, j0:j1, :, :].rearrange("p t m j -> p (t m j)"),
+                )
 
         def h_pass(g, j):
             nc.tensor.matmul_mx(
@@ -172,118 +161,113 @@ def tile_mix_three_fm_bias_kernel(
                 stop=(g == NK - 1),
             )
 
-        def where(n):
-            c = P * n
-            s = 0 if c < 512 else (1 if c < 1024 else 2)
-            return s, c - SECTIONS[s][0]
+        parked = range(EARLY - PACK)
 
-        def y_pass(n, g, t0=0, t1=T):
-            s, c = where(n)
-            ss, cc = (0, P * n) if s == 0 else (1, P * n - 512)
+        def y_pass(n, g):
+            s = 0 if n < BANKS else (1 if n < EARLY else 2)
+            c = P * (n - SECTIONS[s][0])
             if g < NO:
                 lhsT = w8[s][:, g, c : c + P].bitcast(E4M3)
-                lscale = w8s[4 + 4 * g : P, P * n : P * (n + 1)]
+                lscale = w8s[4:P, g, P * n : P * (n + 1)]
             else:
                 lhsT = w4[s][:, g - NO, 2 * c : 2 * (c + P)].bitcast(E2M1)
-                lscale = w4s[ss][:, g - NO, cc : cc + P]
+                lscale = w4s[:, g - NO, P * n : P * (n + 1)]
             nc.tensor.matmul_mx(
                 out=y_acc[n][:], lhsT=lhsT, lhsT_scale=lscale,
-                rhs=x_codes[g][:, t0:t1].bitcast(E4M3), rhs_scale=x_scale[g][:, t0:t1],
-                start=(g == 0), stop=False,
+                rhs=x_codes[g][:].bitcast(E4M3), rhs_scale=x_scale[g][:],
+                start=(g == 0), stop=(g == NK - 1 and n in parked),
             )
 
-        def up_pass(n, t0=0, t1=T):
+        def up_pass(n):
             nc.tensor.matmul_mx(
                 out=y_acc[n][:],
                 lhsT=up[:, 2 * P * n : 2 * P * (n + 1)].bitcast(E2M1), lhsT_scale=ups[:, P * n : P * (n + 1)],
-                rhs=h_codes[:, t0:t1].bitcast(E4M3), rhs_scale=h_scale[:, t0:t1],
-                start=False, stop=True,
+                rhs=h_codes[:].bitcast(E4M3), rhs_scale=h_scale[:],
+                start=(n in parked), stop=True,
             )
 
-        def finish(n):
-            o = res.tile([P, T], F32, name="o")
-            if n % 2 == 0:
-                nc.scalar.activation(out=o[:], in_=y_acc[n][:], func=IDENT, bias=b_col[:, n : n + 1])
+        def add_bias(n, on_scalar):
+            if on_scalar:
+                nc.scalar.activation(out=res[n][:], in_=y_acc[n][:], func=IDENT, bias=b_col[:, n : n + 1])
             else:
-                nc.vector.tensor_scalar_add(o[:], y_acc[n][:], b_col[:, n : n + 1])
-            nc.sync.dma_start(out=out[P * n : P * (n + 1), :], in_=o[:])
+                nc.vector.tensor_scalar_add(res[n][:], y_acc[n][:], b_col[:, n : n + 1])
 
         y_acc = {}
+        bank_of = {}
 
-        def open_bank(n):
-            y_acc[n] = psum.tile([P, T], F32, name=f"bank{n % 8}")
+        def open_bank(n, bank):
+            bank_of[n] = bank
+            y_acc[n] = psum.tile([P, T], F32, name=f"bank{bank}")
 
-        b_turn = psum.tile([P, P], F32, name="bank0")
+        b_turn = psum.tile([P, P], F32, name=f"bank{BANKS - 1}")
         nc.tensor.transpose(b_turn[:], b_rows[:], ident[:])
-        h_acc = [psum.tile([P, T], F32, name=f"bank{4 + j}") for j in range(PACK)]
-        for g in range(3):
+        nc.scalar.activation(out=b_col[:], in_=b_turn[:, 0:NT], func=IDENT)
+
+        for n in range(BANKS):
+            open_bank(n, n)
+        for g in range(NK):
             quant_x(g)
-            if g == 0:
-                nc.scalar.copy(out=b_col[:], in_=b_turn[:, 0:NT])
-            d_grp = group.tile([P, PACK, P, PACK], BF16, name="d_grp", align_bytes=64)
-            spread_d(g, d_grp, 0, P)
-            quant_d(g, d_grp, 0, 4)
+            for n in range(BANKS):
+                y_pass(n, g)
+        for n in parked[: EARLY - BANKS]:
+            add_bias(n, n % 2 == 0)
+        d_grp = spread_d(0)
+        for n in parked[EARLY - BANKS : -1]:
+            add_bias(n, n % 2 == 0)
+        quant_d(0, d_grp, 1)
+        add_bias(parked[-1], parked[-1] % 2 == 0)
+        for n in range(BANKS, EARLY):
+            open_bank(n, n - BANKS)
+        h_banks = range(EARLY - BANKS, EARLY - BANKS + PACK)
+        h_acc = [psum.tile([P, T], F32, name=f"bank{bank}") for bank in h_banks]
+        for n in range(BANKS, EARLY):
+            y_pass(n, 0)
+        for g in range(NK):
+            if g > 0:
+                quant_d(g, spread_d(g), PACK if g == NK - 1 else 1)
+            if g < NK - 1:
+                for n in range(BANKS, EARLY):
+                    y_pass(n, g + 1)
             for j in range(PACK):
                 h_pass(g, j)
-        for n in range(4):
-            open_bank(n)
-        for g in range(3):
-            for n in range(4):
-                y_pass(n, g)
-        quant_x(3)
-        for n in range(4):
-            y_pass(n, 3)
-        quant_x(4)
-        for n in range(4):
-            y_pass(n, 4)
-        d_grp = group.tile([P, PACK, P, PACK], BF16, name="d_grp", align_bytes=64)
-        spread_d(3, d_grp, 0, P)
-        quant_d(3, d_grp, 0, 4)
-        for j in range(PACK):
-            h_pass(3, j)
-        d_grp = group.tile([P, PACK, P, PACK], BF16, name="d_grp", align_bytes=64)
-        spread_d(4, d_grp, 0, P)
-        for j in range(PACK):
-            quant_d(4, d_grp, j, j + 1)
-        for j in range(PACK):
-            h_pass(4, j)
         for j in range(PACK):
             copy = nc.scalar.copy if j % 2 == 0 else nc.vector.tensor_copy
             copy(out=h_rows[:, j, :], in_=h_acc[j][:])
-        for n in range(4, 8):
-            open_bank(n)
-        for g in range(NO):
-            for n in range(4, 8):
-                y_pass(n, g)
         for copy, c0, c1 in ((nc.vector.tensor_copy, 0, 320), (nc.scalar.copy, 320, T)):
             copy(out=h_grp[:, c0:c1, :], in_=h_rows[:, :, c0:c1].rearrange("p j t -> p t j"))
         nc.vector.quantize_mx(
             out=h_codes[:].bitcast(E4M3), scales=h_scale[:], in_=h_grp[:].rearrange("p t j -> p (t j)")
         )
-        for n in range(4, 8):
-            for g in range(NO, NK):
-                y_pass(n, g)
-        for n in range(8):
-            up_pass(n)
-            finish(n)
-        for n in range(8, NT - 1):
-            open_bank(n)
-            for g in range(NK):
-                y_pass(n, g)
-            up_pass(n)
-            finish(n)
-        n = NT - 1
-        o = res.tile([P, T], F32, name="o")
-        for q in range(4):
-            y_acc[n] = psum.tile([P, P], F32, name=f"bank{q}")
-            for g in range(NK):
-                y_pass(n, g, P * q, P * (q + 1))
-            up_pass(n, P * q, P * (q + 1))
-            t0, t1 = P * q, P * (q + 1)
-            if q % 2 == 1:
-                nc.scalar.activation(out=o[:, t0:t1], in_=y_acc[n][:], func=IDENT, bias=b_col[:, n : n + 1])
+        late = [(n, g) for n in range(EARLY, NT) for g in range(NK)]
+        whole = list(range(EARLY - PACK, NT))
+        free = [h_banks[0], h_banks[1]]
+
+        def late_pass():
+            n, g = late[0]
+            late.remove((n, g))
+            if g == 0:
+                open_bank(n, free[0])
+                free.remove(free[0])
+            y_pass(n, g)
+
+        for i in range(GAP_PASSES):
+            late_pass()
+        order = []
+        for i in range(len(whole)):
+            order.append(whole[i])
+            if i < len(parked):
+                order.append(parked[i])
+        for n in order:
+            if n in parked:
+                open_bank(n, h_banks[2 + n % 2])
+                up_pass(n)
+                nc.vector.tensor_add(res[n][:], y_acc[n][:], res[n][:])
             else:
-                nc.vector.tensor_scalar_add(o[:, t0:t1], y_acc[n][:], b_col[:, n : n + 1])
-            if q > 0:
-                s0 = 0 if q == 1 else t0
-                nc.sync.dma_start(out=out[P * n : P * (n + 1), s0:t1], in_=o[:, s0:t1])
+                while any(m == n for m, g in late):
+                    late_pass()
+                up_pass(n)
+                add_bias(n, True)
+                free.append(bank_of[n])
+            nc.sync.dma_start(out=out[P * n : P * (n + 1), :], in_=res[n][:])
+            if late:
+                late_pass()

@@ -22,10 +22,12 @@ NK = K // KP
 NO = O // KP
 NT = M // P
 BANKS = 8
-EARLY = 12
-SECTIONS = ((0, BANKS), (BANKS, EARLY), (EARLY, NT))
+HELD = BANKS - PACK
+LAST = NO - 1
+SECTIONS = ((0, 4), (4, BANKS), (BANKS, NT))
+GAP_PARKED = 2
 XV = 256
-GAP_PASSES = 8
+XV_LAST = 160
 
 
 def tile_mix_three_fm_bias_kernel(
@@ -38,35 +40,34 @@ def tile_mix_three_fm_bias_kernel(
         psum = ctx.enter_context(tc.psum_pool(name="psum", bufs=1))
         ctx.enter_context(tc.manual_schedule())
 
-        x_raw = [keep.tile([P, PACK, T], F32, name=f"x_raw{g}") for g in range(NK)]
+        x_raw = {g: keep.tile([P, PACK, T], F32, name=f"x_raw{g}") for g in range(NK) if g != LAST}
+        x_last = [keep.tile([P, PACK, T // 2], F32, name=f"x_last{half}") for half in range(2)]
         d_raw = [keep.tile([P, PACK, R], F32, name=f"d_raw{g}") for g in range(NK)]
         x_codes = [keep.tile([P, T], U32, name=f"x_codes{g}", align_bytes=64) for g in range(NK)]
         x_scale = [keep.tile([P, T], U8, name=f"x_scale{g}", align_bytes=64) for g in range(NK)]
         d_codes = [keep.tile([P, R], U32, name=f"d_codes{g}", align_bytes=64) for g in range(NK)]
         d_scale = [keep.tile([P, R], U8, name=f"d_scale{g}", align_bytes=64) for g in range(NK)]
         w8 = [keep.tile([P, NO, P * (n1 - n0)], U32, name=f"w8_{n0}", align_bytes=64) for n0, n1 in SECTIONS]
-        w4 = [keep.tile([P, NK - NO, 2 * P * (n1 - n0)], U8, name=f"w4_{n0}", align_bytes=64) for n0, n1 in SECTIONS]
-        w8s = keep.tile([P, NO, M], U8, name="w8s", align_bytes=64)
+        w4 = [keep.tile([P, NK - NO, M], U8, name=f"w4_{s}", align_bytes=64) for s in range(2)]
+        w8s = keep.tile([P, M], U8, name="w8s", align_bytes=64)
         w4s = keep.tile([P, NK - NO, M], U8, name="w4s", align_bytes=64)
         up = keep.tile([P, 2 * M], U8, name="up", align_bytes=64)
         ups = keep.tile([P, M], U8, name="ups", align_bytes=64)
         b_rows = keep.tile([P, P], F32, name="b_rows")
         ident = keep.tile([P, P], F32, name="ident")
         b_col = keep.tile([P, NT], F32, name="b_col")
-        h_rows = keep.tile([P, PACK, T], BF16, name="h_rows", align_bytes=64)
         h_grp = keep.tile([P, T, PACK], BF16, name="h_grp", align_bytes=64)
         h_codes = keep.tile([P, T], U32, name="h_codes", align_bytes=64)
         h_scale = keep.tile([P, T], U8, name="h_scale", align_bytes=64)
         res = [keep.tile([P, T], F32, name=f"res{n}") for n in range(NT)]
 
         nc.gpsimd.memset(b_rows[:], 0.0)
-        nc.vector.memset(w8s[:].rearrange("p a n -> p (a n)").bitcast(I32), 0)
         nc.vector.memset(w4s[:].rearrange("p a n -> p (a n)").bitcast(I32), 0)
+        nc.vector.memset(w8s[:].bitcast(I32), 0)
         nc.vector.memset(ups[:].bitcast(I32), 0)
         make_identity(nc, ident[:])
 
         w8_view = w8_words.rearrange("a p n i -> p a (n i)")
-        w4_view = w4_words.rearrange("a p n -> p a n")
 
         def load_x(g):
             nc.sync.dma_start(
@@ -80,102 +81,111 @@ def tile_mix_three_fm_bias_kernel(
                 in_=down[KP * g : KP * (g + 1), :].rearrange("(p j) r -> p (j r)", j=PACK),
             )
 
-        def load_w8(s, g0=0, g1=NO):
-            n0, n1 = SECTIONS[s]
+        def w8_cols(n0, n1):
+            s = [i for i, (m0, m1) in enumerate(SECTIONS) if m0 <= n0 < m1][0]
+            return w8[s][:, :, P * (n0 - SECTIONS[s][0]) : P * (n1 - SECTIONS[s][0])]
+
+        def load_w8(n0, n1, g0, g1):
             nc.sync.dma_start(
-                out=w8[s][:, g0:g1, :].bitcast(I32), in_=w8_view[:, g0:g1, 4 * P * n0 : 4 * P * n1].bitcast(I32)
+                out=w8_cols(n0, n1)[:, g0:g1, :].bitcast(I32),
+                in_=w8_view[:, g0:g1, 4 * P * n0 : 4 * P * n1].bitcast(I32),
             )
 
-        def load_w4(s, g0=NO, g1=NK):
-            n0, n1 = SECTIONS[s]
-            nc.sync.dma_start(
-                out=w4[s][:, g0 - NO : g1 - NO, :].bitcast(I32),
-                in_=w4_view[:, g0 - NO : g1 - NO, 2 * P * n0 : 2 * P * n1].bitcast(I32),
-            )
-
-        def load_scales(eng, plane, scales, first):
-            rows = scales.rearrange("a q n -> q a n")
+        def load_w4s():
+            rows = w4_scales.rearrange("a q n -> q a n")
             for r in range(4):
-                eng.dma_start(out=plane[first + r : P : 32].bitcast(I32), in_=rows[r:16:4].bitcast(I32))
+                nc.gpsimd.dma_start(out=w4s[r:P:32].bitcast(I32), in_=rows[r:16:4].bitcast(I32))
 
-        load_x(0)
-        nc.sync.dma_start(out=b_rows[0:NT, :], in_=b.rearrange("(g p) -> g p", p=P))
-        load_scales(nc.sync, w8s, w8_scales, 4)
-        load_w8(0, 0, 1)
-        load_x(1)
-        load_w8(0, 1, 2)
-        load_x(2)
-        load_scales(nc.sync, w4s, w4_scales, 0)
-        load_w4(0, 2, 3)
-        for g in (3, 4):
+        def load_w8s():
+            for q in range(4):
+                nc.gpsimd.dma_start(
+                    out=w8s[32 * q + 4 : 32 * q + 12, :].bitcast(I32),
+                    in_=w8_scales[:, 4 * q : 4 * q + 4, :].bitcast(I32),
+                )
+
+        for g in range(NO, NK):
             load_x(g)
-            load_w4(0, g, g + 1)
-        load_w8(1)
-        load_w4(1)
-        for g in range(NK):
+            if g == NO:
+                nc.sync.dma_start(out=b_rows[0:NT, :], in_=b.rearrange("(g p) -> g p", p=P))
+                load_w4s()
+                load_w8s()
+            nc.sync.dma_start(out=w4[0][:, g - NO, :].bitcast(I32), in_=w4_words[g - NO, :, 0:M].bitcast(I32))
+        nc.sync.dma_start(out=w4[1][:].bitcast(I32), in_=w4_words.rearrange("a p n -> p a n")[:, :, M:].bitcast(I32))
+        load_x(0)
+        load_w8(BANKS, NT - HELD, 0, 1)
+        d_order = [g for g in range(NK) if g != LAST] + [LAST]
+        for g in d_order:
             load_d(g)
-        load_w8(2)
-        load_w4(2)
-        nc.sync.dma_start(out=up[:].bitcast(I32), in_=up_words[0].bitcast(I32))
+        load_w8(NT - HELD, NT, 0, 1)
+        x_rows = x[KP * LAST : KP * (LAST + 1), :].rearrange("(p j) t -> p j t", j=PACK)
+        for half in range(2):
+            nc.sync.dma_start(out=x_last[half][:], in_=x_rows[:, :, half * T // 2 : (half + 1) * T // 2])
+        load_w8(BANKS, NT, LAST, NO)
         for r in range(4):
             nc.sync.dma_start(out=ups[r:P:32, :].bitcast(I32), in_=up_scales[0, r:16:4, :].bitcast(I32))
+        nc.sync.dma_start(out=up[:].bitcast(I32), in_=up_words[0].bitcast(I32))
+        for n0, n1 in SECTIONS[:2]:
+            load_w8(n0, n1, 0, NO)
 
-        def quant_x(g):
-            grp = group.tile([P, T, PACK], BF16, name="x_grp", align_bytes=64)
-            for copy, c0, c1 in ((nc.vector.tensor_copy, 0, XV), (nc.scalar.copy, XV, T)):
+        def spread_x(raw, split):
+            width = raw.shape[2]
+            grp = group.tile([P, width, PACK], BF16, name="x_grp", align_bytes=64)
+            for copy, c0, c1 in ((nc.vector.tensor_copy, 0, split), (nc.scalar.copy, split, width)):
                 copy(
                     out=grp[:, c0:c1, :].rearrange("p (c i) j -> p c j i", i=4),
-                    in_=x_raw[g][:, :, c0:c1].rearrange("p j (c i) -> p c j i", i=4),
+                    in_=raw[:, :, c0:c1].rearrange("p j (c i) -> p c j i", i=4),
                 )
+            return grp
+
+        def quant_x(g, grp, t0=0, t1=T):
             nc.vector.quantize_mx(
-                out=x_codes[g][:].bitcast(E4M3), scales=x_scale[g][:], in_=grp[:].rearrange("p t j -> p (t j)")
+                out=x_codes[g][:, t0:t1].bitcast(E4M3),
+                scales=x_scale[g][:, t0:t1],
+                in_=grp[:].rearrange("p t j -> p (t j)"),
             )
 
-        def spread_d(g):
+        def quant_d(g):
             grp = group.tile([P, PACK, P, PACK], BF16, name="d_grp", align_bytes=64)
             for copy, j0, j1 in ((nc.vector.tensor_copy, 0, 2), (nc.scalar.copy, 2, 4)):
                 copy(
                     out=grp[:, j0:j1, :, :].rearrange("p t m j -> p m j t"),
                     in_=d_raw[g][:].rearrange("p j (m t) -> p m j t", t=4)[:, :, :, j0:j1],
                 )
-            return grp
-
-        def quant_d(g, grp, parts):
-            width = PACK // parts
-            for j0 in range(0, PACK, width):
-                j1 = j0 + width
+            for j0, j1 in ((0, 2), (2, 4)):
                 nc.vector.quantize_mx(
                     out=d_codes[g][:, P * j0 : P * j1].bitcast(E4M3),
                     scales=d_scale[g][:, P * j0 : P * j1],
                     in_=grp[:, j0:j1, :, :].rearrange("p t m j -> p (t m j)"),
                 )
 
-        def h_pass(g, j):
+        def h_pass(g, j, q):
             nc.tensor.matmul_mx(
-                out=h_acc[j][:],
+                out=h_acc[q][:, j, :],
                 lhsT=d_codes[g][:, P * j : P * (j + 1)].bitcast(E4M3),
                 lhsT_scale=d_scale[g][:, P * j : P * (j + 1)],
-                rhs=x_codes[g][:].bitcast(E4M3),
-                rhs_scale=x_scale[g][:],
-                start=(g == 0),
-                stop=(g == NK - 1),
+                rhs=x_codes[g][:, P * q : P * (q + 1)].bitcast(E4M3),
+                rhs_scale=x_scale[g][:, P * q : P * (q + 1)],
+                start=(g == 0 and j == 0),
+                stop=(g == LAST and j == PACK - 1),
             )
 
-        parked = range(EARLY - PACK)
-
-        def y_pass(n, g):
-            s = 0 if n < BANKS else (1 if n < EARLY else 2)
-            c = P * (n - SECTIONS[s][0])
-            if g < NO:
-                lhsT = w8[s][:, g, c : c + P].bitcast(E4M3)
-                lscale = w8s[4:P, g, P * n : P * (n + 1)]
-            else:
-                lhsT = w4[s][:, g - NO, 2 * c : 2 * (c + P)].bitcast(E2M1)
-                lscale = w4s[:, g - NO, P * n : P * (n + 1)]
+        def w4_pass(n, g):
             nc.tensor.matmul_mx(
-                out=y_acc[n][:], lhsT=lhsT, lhsT_scale=lscale,
+                out=y_acc[n][:],
+                lhsT=w4[n // BANKS][:, g - NO, 2 * P * (n % BANKS) : 2 * P * (n % BANKS + 1)].bitcast(E2M1),
+                lhsT_scale=w4s[:, g - NO, P * n : P * (n + 1)],
                 rhs=x_codes[g][:].bitcast(E4M3), rhs_scale=x_scale[g][:],
-                start=(g == 0), stop=(g == NK - 1 and n in parked),
+                start=(g == NO), stop=(g == NK - 1 and n < BANKS),
+            )
+
+        def w8_pass(n, g):
+            nc.tensor.matmul_mx(
+                out=y_acc[n][:],
+                lhsT=w8_cols(n, n + 1)[:, g, :].bitcast(E4M3),
+                lhsT_scale=w8s[4 + 4 * g : P, P * n : P * (n + 1)],
+                rhs=x_codes[g][:].bitcast(E4M3), rhs_scale=x_scale[g][:],
+                start=(n < NT - HELD and g == (0 if n < BANKS else LAST)),
+                stop=(g == 0 and BANKS <= n < NT - HELD),
             )
 
         def up_pass(n):
@@ -183,7 +193,7 @@ def tile_mix_three_fm_bias_kernel(
                 out=y_acc[n][:],
                 lhsT=up[:, 2 * P * n : 2 * P * (n + 1)].bitcast(E2M1), lhsT_scale=ups[:, P * n : P * (n + 1)],
                 rhs=h_codes[:].bitcast(E4M3), rhs_scale=h_scale[:],
-                start=(n in parked), stop=True,
+                start=False, stop=True,
             )
 
         def add_bias(n, on_scalar):
@@ -205,69 +215,89 @@ def tile_mix_three_fm_bias_kernel(
 
         for n in range(BANKS):
             open_bank(n, n)
-        for g in range(NK):
-            quant_x(g)
+        for g in range(NO, NK):
+            quant_x(g, spread_x(x_raw[g], XV))
             for n in range(BANKS):
-                y_pass(n, g)
-        for n in parked[: EARLY - BANKS]:
+                w4_pass(n, g)
+        for n in range(HELD):
             add_bias(n, n % 2 == 0)
-        d_grp = spread_d(0)
-        for n in parked[EARLY - BANKS : -1]:
+        grp = spread_x(x_raw[0], XV)
+        for n in range(HELD, BANKS - 1):
             add_bias(n, n % 2 == 0)
-        quant_d(0, d_grp, 1)
-        add_bias(parked[-1], parked[-1] % 2 == 0)
-        for n in range(BANKS, EARLY):
-            open_bank(n, n - BANKS)
-        h_banks = range(EARLY - BANKS, EARLY - BANKS + PACK)
-        h_acc = [psum.tile([P, T], F32, name=f"bank{bank}") for bank in h_banks]
-        for n in range(BANKS, EARLY):
-            y_pass(n, 0)
-        for g in range(NK):
-            if g > 0:
-                quant_d(g, spread_d(g), PACK if g == NK - 1 else 1)
-            if g < NK - 1:
-                for n in range(BANKS, EARLY):
-                    y_pass(n, g + 1)
-            for j in range(PACK):
-                h_pass(g, j)
-        for j in range(PACK):
-            copy = nc.scalar.copy if j % 2 == 0 else nc.vector.tensor_copy
-            copy(out=h_rows[:, j, :], in_=h_acc[j][:])
-        for copy, c0, c1 in ((nc.vector.tensor_copy, 0, 320), (nc.scalar.copy, 320, T)):
-            copy(out=h_grp[:, c0:c1, :], in_=h_rows[:, :, c0:c1].rearrange("p j t -> p t j"))
-        nc.vector.quantize_mx(
-            out=h_codes[:].bitcast(E4M3), scales=h_scale[:], in_=h_grp[:].rearrange("p t j -> p (t j)")
-        )
-        late = [(n, g) for n in range(EARLY, NT) for g in range(NK)]
-        whole = list(range(EARLY - PACK, NT))
-        free = [h_banks[0], h_banks[1]]
+        quant_x(0, grp)
+        add_bias(BANKS - 1, False)
 
-        def late_pass():
-            n, g = late[0]
-            late.remove((n, g))
-            if g == 0:
+        def early_tile(n):
+            open_bank(n, n % HELD)
+            for g in range(NO, NK):
+                w4_pass(n, g)
+
+        def h_passes(g, quarters):
+            for q in quarters:
+                for j in range(PACK):
+                    h_pass(g, j, q)
+
+        for n in range(BANKS, NT - HELD):
+            early_tile(n)
+        quant_d(d_order[0])
+        for n in range(BANKS, NT - HELD):
+            w8_pass(n, 0)
+            add_bias(n, True)
+        quant_d(d_order[1])
+        h_banks = range(HELD, BANKS)
+        h_acc = [psum.tile([P, PACK, P], F32, name=f"bank{bank}") for bank in h_banks]
+        for i, g in enumerate(d_order[:-1]):
+            h_passes(g, range(PACK))
+            early_tile(NT - HELD + i)
+            if i + 2 < NK:
+                quant_d(d_order[i + 2])
+        for n in range(NT - HELD, NT):
+            w8_pass(n, 0)
+
+        def spread_h(copy, q):
+            copy(out=h_grp[:, P * q : P * (q + 1), :], in_=h_acc[q][:].rearrange("p j t -> p t j"))
+
+        def quant_h(q):
+            t0, t1 = P * q, P * (q + 1)
+            nc.vector.quantize_mx(
+                out=h_codes[:, t0:t1].bitcast(E4M3),
+                scales=h_scale[:, t0:t1],
+                in_=h_grp[:, t0:t1, :].rearrange("p t j -> p (t j)"),
+            )
+
+        for half in range(2):
+            quant_x(LAST, spread_x(x_last[half], XV_LAST), half * T // 2, (half + 1) * T // 2)
+            h_passes(LAST, (2 * half, 2 * half + 1))
+        for q in (0, 2):
+            spread_h(nc.scalar.copy, q)
+            spread_h(nc.vector.tensor_copy, q + 1)
+            quant_h(q)
+            quant_h(q + 1)
+
+        free = list(h_banks)
+
+        def late_passes(n):
+            if n < NT - HELD:
                 open_bank(n, free[0])
                 free.remove(free[0])
-            y_pass(n, g)
+            for g in range(0 if n < BANKS else LAST, NO):
+                w8_pass(n, g)
 
-        for i in range(GAP_PASSES):
-            late_pass()
-        order = []
-        for i in range(len(whole)):
-            order.append(whole[i])
-            if i < len(parked):
-                order.append(parked[i])
+        held = list(range(NT - HELD, NT))
+        ahead = held + list(range(BANKS, BANKS + GAP_PARKED))
+        for n in ahead:
+            late_passes(n)
+        order = [n for pair in zip(held, range(BANKS, NT - HELD)) for n in pair] + list(range(BANKS))
         for n in order:
-            if n in parked:
-                open_bank(n, h_banks[2 + n % 2])
-                up_pass(n)
-                nc.vector.tensor_add(res[n][:], y_acc[n][:], res[n][:])
-            else:
-                while any(m == n for m, g in late):
-                    late_pass()
-                up_pass(n)
-                add_bias(n, True)
-                free.append(bank_of[n])
-            nc.sync.dma_start(out=out[P * n : P * (n + 1), :], in_=res[n][:])
-            if late:
-                late_pass()
+            if n not in ahead:
+                late_passes(n)
+            up_pass(n)
+            halves = 2 if n == order[-1] else 1
+            for half in range(halves):
+                cols = slice(half * T // halves, (half + 1) * T // halves)
+                if n in held:
+                    add_bias(n, True)
+                else:
+                    nc.vector.tensor_add(res[n][:, cols], y_acc[n][:, cols], res[n][:, cols])
+                nc.sync.dma_start(out=out[P * n : P * (n + 1), cols], in_=res[n][:, cols])
+            free.append(bank_of[n])

@@ -49,7 +49,7 @@ def tile_mix_three_fm_bias_kernel(
         d_scale = [keep.tile([P, R], U8, name=f"d_scale{g}", align_bytes=64) for g in range(NK)]
         w8 = [keep.tile([P, NO, P * (n1 - n0)], U32, name=f"w8_{n0}", align_bytes=64) for n0, n1 in SECTIONS]
         w4 = [keep.tile([P, NK - NO, M], U8, name=f"w4_{s}", align_bytes=64) for s in range(2)]
-        w8s = keep.tile([P, M], U8, name="w8s", align_bytes=64)
+        w8s = [keep.tile([P, M // 2], U8, name=f"w8s_{i}", align_bytes=64) for i in range(3)]
         w4s = keep.tile([P, NK - NO, M], U8, name="w4s", align_bytes=64)
         up = keep.tile([P, 2 * M], U8, name="up", align_bytes=64)
         ups = keep.tile([P, M], U8, name="ups", align_bytes=64)
@@ -63,7 +63,8 @@ def tile_mix_three_fm_bias_kernel(
 
         nc.gpsimd.memset(b_rows[:], 0.0)
         nc.vector.memset(w4s[:].rearrange("p a n -> p (a n)").bitcast(I32), 0)
-        nc.vector.memset(w8s[:].bitcast(I32), 0)
+        for plane in w8s:
+            nc.vector.memset(plane[:].bitcast(I32), 0)
         nc.vector.memset(ups[:].bitcast(I32), 0)
         make_identity(nc, ident[:])
 
@@ -94,13 +95,20 @@ def tile_mix_three_fm_bias_kernel(
         def load_w4s():
             rows = w4_scales.rearrange("a q n -> q a n")
             for r in range(4):
-                nc.gpsimd.dma_start(out=w4s[r:P:32].bitcast(I32), in_=rows[r:16:4].bitcast(I32))
+                nc.sync.dma_start(out=w4s[r:P:32].bitcast(I32), in_=rows[r:16:4].bitcast(I32))
 
-        def load_w8s():
+        def load_w8s_upper(queue, g):
+            for r in range(4):
+                queue.dma_start(
+                    out=w8s[1 + g][4 + 4 * g + r : P : 32, :].bitcast(I32),
+                    in_=w8_scales[g, r:16:4, M // 2 : M].bitcast(I32),
+                )
+
+        def load_w8s_lower():
             for q in range(4):
                 nc.gpsimd.dma_start(
-                    out=w8s[32 * q + 4 : 32 * q + 12, :].bitcast(I32),
-                    in_=w8_scales[:, 4 * q : 4 * q + 4, :].bitcast(I32),
+                    out=w8s[0][32 * q + 4 : 32 * q + 12, :].bitcast(I32),
+                    in_=w8_scales[:, 4 * q : 4 * q + 4, 0 : M // 2].bitcast(I32),
                 )
 
         for g in range(NO, NK):
@@ -108,10 +116,12 @@ def tile_mix_three_fm_bias_kernel(
             if g == NO:
                 nc.sync.dma_start(out=b_rows[0:NT, :], in_=b.rearrange("(g p) -> g p", p=P))
                 load_w4s()
-                load_w8s()
+                load_w8s_upper(nc.gpsimd, LAST)
+                load_w8s_lower()
             nc.sync.dma_start(out=w4[0][:, g - NO, :].bitcast(I32), in_=w4_words[g - NO, :, 0:M].bitcast(I32))
         nc.sync.dma_start(out=w4[1][:].bitcast(I32), in_=w4_words.rearrange("a p n -> p a n")[:, :, M:].bitcast(I32))
         load_x(0)
+        load_w8s_upper(nc.sync, 0)
         load_w8(BANKS, NT - HELD, 0, 1)
         d_order = [g for g in range(NK) if g != LAST] + [LAST]
         for g in d_order:
@@ -182,7 +192,7 @@ def tile_mix_three_fm_bias_kernel(
             nc.tensor.matmul_mx(
                 out=y_acc[n][:],
                 lhsT=w8_cols(n, n + 1)[:, g, :].bitcast(E4M3),
-                lhsT_scale=w8s[4 + 4 * g : P, P * n : P * (n + 1)],
+                lhsT_scale=w8s[0 if n < BANKS else 1 + g][4 + 4 * g : P, P * (n % BANKS) : P * (n % BANKS + 1)],
                 rhs=x_codes[g][:].bitcast(E4M3), rhs_scale=x_scale[g][:],
                 start=(n < NT - HELD and g == (0 if n < BANKS else LAST)),
                 stop=(g == 0 and BANKS <= n < NT - HELD),

@@ -17,17 +17,20 @@ IDENT = mybir.ActivationFunctionType.Identity
 
 P = 128
 PACK = 4
-KP = 512
+KP = P * PACK
 NK = K // KP
 NO = O // KP
 NT = M // P
 BANKS = 8
-HELD = BANKS - PACK
+QUARTERS = T // P
+HELD = BANKS - QUARTERS
+FIRST_HELD = NT - HELD
 LAST = NO - 1
-SECTIONS = ((0, 4), (4, BANKS), (BANKS, NT))
-GAP_PARKED = 2
-XV = 256
-XV_LAST = 160
+LATE = HELD
+W8_PARTS = ((0, LATE), (LATE, NT))
+FILL = 2
+X_VECTOR = 320
+X_VECTOR_HALF = 160
 
 
 def tile_mix_three_fm_bias_kernel(
@@ -47,10 +50,13 @@ def tile_mix_three_fm_bias_kernel(
         x_scale = [keep.tile([P, T], U8, name=f"x_scale{g}", align_bytes=64) for g in range(NK)]
         d_codes = [keep.tile([P, R], U32, name=f"d_codes{g}", align_bytes=64) for g in range(NK)]
         d_scale = [keep.tile([P, R], U8, name=f"d_scale{g}", align_bytes=64) for g in range(NK)]
-        w8 = [keep.tile([P, NO, P * (n1 - n0)], U32, name=f"w8_{n0}", align_bytes=64) for n0, n1 in SECTIONS]
-        w4 = [keep.tile([P, NK - NO, M], U8, name=f"w4_{s}", align_bytes=64) for s in range(2)]
-        w8s = [keep.tile([P, M // 2], U8, name=f"w8s_{i}", align_bytes=64) for i in range(3)]
-        w4s = keep.tile([P, NK - NO, M], U8, name="w4s", align_bytes=64)
+        w8 = [keep.tile([P, NO, P * (n1 - n0)], U32, name=f"w8_{n0}", align_bytes=64) for n0, n1 in W8_PARTS]
+        w4 = [keep.tile([P, NK - NO, M], U8, name=f"w4_{half}", align_bytes=64) for half in range(2)]
+        w8s = [
+            keep.tile([P, width], U8, name=f"w8s_{i}", align_bytes=64)
+            for i, width in enumerate((P * LATE, M - P * LATE, M - P * LATE))
+        ]
+        w4s = [keep.tile([P, NK - NO, M // 2], U8, name=f"w4s_{half}", align_bytes=64) for half in range(2)]
         up = keep.tile([P, 2 * M], U8, name="up", align_bytes=64)
         ups = keep.tile([P, M], U8, name="ups", align_bytes=64)
         b_rows = keep.tile([P, P], F32, name="b_rows")
@@ -62,71 +68,65 @@ def tile_mix_three_fm_bias_kernel(
         res = [keep.tile([P, T], F32, name=f"res{n}") for n in range(NT)]
 
         nc.gpsimd.memset(b_rows[:], 0.0)
-        nc.vector.memset(w4s[:].rearrange("p a n -> p (a n)").bitcast(I32), 0)
+        nc.vector.memset(w4s[0][:].rearrange("p a n -> p (a n)").bitcast(I32), 0)
         for plane in w8s:
             nc.vector.memset(plane[:].bitcast(I32), 0)
+        nc.vector.memset(w4s[1][:].rearrange("p a n -> p (a n)").bitcast(I32), 0)
         nc.vector.memset(ups[:].bitcast(I32), 0)
         make_identity(nc, ident[:])
 
         w8_view = w8_words.rearrange("a p n i -> p a (n i)")
 
-        def load_x(g):
+        def load_pass(raw, source, g):
             nc.sync.dma_start(
-                out=x_raw[g][:].rearrange("p j t -> p (j t)"),
-                in_=x[KP * g : KP * (g + 1), :].rearrange("(p j) t -> p (j t)", j=PACK),
-            )
-
-        def load_d(g):
-            nc.sync.dma_start(
-                out=d_raw[g][:].rearrange("p j r -> p (j r)"),
-                in_=down[KP * g : KP * (g + 1), :].rearrange("(p j) r -> p (j r)", j=PACK),
+                out=raw[:].rearrange("p j c -> p (j c)"),
+                in_=source[KP * g : KP * (g + 1), :].rearrange("(p j) c -> p (j c)", j=PACK),
             )
 
         def w8_cols(n0, n1):
-            s = [i for i, (m0, m1) in enumerate(SECTIONS) if m0 <= n0 < m1][0]
-            return w8[s][:, :, P * (n0 - SECTIONS[s][0]) : P * (n1 - SECTIONS[s][0])]
+            part = 0 if n0 < LATE else 1
+            first = W8_PARTS[part][0]
+            return w8[part][:, :, P * (n0 - first) : P * (n1 - first)]
 
         def load_w8(n0, n1, g0, g1):
             nc.sync.dma_start(
                 out=w8_cols(n0, n1)[:, g0:g1, :].bitcast(I32),
-                in_=w8_view[:, g0:g1, 4 * P * n0 : 4 * P * n1].bitcast(I32),
+                in_=w8_view[:, g0:g1, PACK * P * n0 : PACK * P * n1].bitcast(I32),
             )
 
-        def load_w4s():
-            rows = w4_scales.rearrange("a q n -> q a n")
+        def load_w4s(half):
+            rows = w4_scales.rearrange("a q n -> q a n")[:, :, half * M // 2 : (half + 1) * M // 2]
             for r in range(4):
-                nc.sync.dma_start(out=w4s[r:P:32].bitcast(I32), in_=rows[r:16:4].bitcast(I32))
+                nc.sync.dma_start(out=w4s[half][r:P:32].bitcast(I32), in_=rows[r:16:4].bitcast(I32))
 
-        def load_w8s_upper(queue, g):
+        def load_w8s(queue, g):
             for r in range(4):
                 queue.dma_start(
                     out=w8s[1 + g][4 + 4 * g + r : P : 32, :].bitcast(I32),
-                    in_=w8_scales[g, r:16:4, M // 2 : M].bitcast(I32),
-                )
-
-        def load_w8s_lower():
-            for q in range(4):
-                nc.gpsimd.dma_start(
-                    out=w8s[0][32 * q + 4 : 32 * q + 12, :].bitcast(I32),
-                    in_=w8_scales[:, 4 * q : 4 * q + 4, 0 : M // 2].bitcast(I32),
+                    in_=w8_scales[g, r:16:4, P * LATE : M].bitcast(I32),
                 )
 
         for g in range(NO, NK):
-            load_x(g)
+            load_pass(x_raw[g], x, g)
             if g == NO:
-                nc.sync.dma_start(out=b_rows[0:NT, :], in_=b.rearrange("(g p) -> g p", p=P))
-                load_w4s()
-                load_w8s_upper(nc.gpsimd, LAST)
-                load_w8s_lower()
+                nc.sync.dma_start(out=b_rows[0:NT, :], in_=b.rearrange("(n p) -> n p", p=P))
+                load_w4s(0)
+                load_w8s(nc.gpsimd, LAST)
+                for quad in range(4):
+                    nc.gpsimd.dma_start(
+                        out=w8s[0][32 * quad + 4 : 32 * quad + 12, :].bitcast(I32),
+                        in_=w8_scales[:, 4 * quad : 4 * quad + 4, 0 : P * LATE].bitcast(I32),
+                    )
             nc.sync.dma_start(out=w4[0][:, g - NO, :].bitcast(I32), in_=w4_words[g - NO, :, 0:M].bitcast(I32))
+        load_w4s(1)
         nc.sync.dma_start(out=w4[1][:].bitcast(I32), in_=w4_words.rearrange("a p n -> p a n")[:, :, M:].bitcast(I32))
-        load_x(0)
-        load_w8s_upper(nc.sync, 0)
-        load_w8(BANKS, NT - HELD, 0, 1)
+        load_pass(x_raw[0], x, 0)
+        load_w8s(nc.sync, 0)
+        load_w8(LATE, FIRST_HELD, 0, 1)
         d_order = [g for g in range(NK) if g != LAST] + [LAST]
         for g in d_order:
-            load_d(g)
-        load_w8(NT - HELD, NT, 0, 1)
+            load_pass(d_raw[g], down, g)
+        load_w8(FIRST_HELD, NT, 0, 1)
         x_rows = x[KP * LAST : KP * (LAST + 1), :].rearrange("(p j) t -> p j t", j=PACK)
         for half in range(2):
             nc.sync.dma_start(out=x_last[half][:], in_=x_rows[:, :, half * T // 2 : (half + 1) * T // 2])
@@ -134,79 +134,86 @@ def tile_mix_three_fm_bias_kernel(
         for r in range(4):
             nc.sync.dma_start(out=ups[r:P:32, :].bitcast(I32), in_=up_scales[0, r:16:4, :].bitcast(I32))
         nc.sync.dma_start(out=up[:].bitcast(I32), in_=up_words[0].bitcast(I32))
-        for n0, n1 in SECTIONS[:2]:
-            load_w8(n0, n1, 0, NO)
+        load_w8(LATE, BANKS, LAST, NO)
+        load_w8(0, LATE, 0, NO)
 
-        def spread_x(raw, split):
+        def quant_x(g, raw, on_vector, t0):
             width = raw.shape[2]
             grp = group.tile([P, width, PACK], BF16, name="x_grp", align_bytes=64)
-            for copy, c0, c1 in ((nc.vector.tensor_copy, 0, split), (nc.scalar.copy, split, width)):
+            for copy, c0, c1 in ((nc.vector.tensor_copy, 0, on_vector), (nc.scalar.copy, on_vector, width)):
                 copy(
                     out=grp[:, c0:c1, :].rearrange("p (c i) j -> p c j i", i=4),
                     in_=raw[:, :, c0:c1].rearrange("p j (c i) -> p c j i", i=4),
                 )
-            return grp
-
-        def quant_x(g, grp, t0=0, t1=T):
             nc.vector.quantize_mx(
-                out=x_codes[g][:, t0:t1].bitcast(E4M3),
-                scales=x_scale[g][:, t0:t1],
+                out=x_codes[g][:, t0 : t0 + width].bitcast(E4M3),
+                scales=x_scale[g][:, t0 : t0 + width],
                 in_=grp[:].rearrange("p t j -> p (t j)"),
             )
 
         def quant_d(g):
             grp = group.tile([P, PACK, P, PACK], BF16, name="d_grp", align_bytes=64)
-            for copy, j0, j1 in ((nc.vector.tensor_copy, 0, 2), (nc.scalar.copy, 2, 4)):
+            for copy, i0, i1 in ((nc.vector.tensor_copy, 0, 2), (nc.scalar.copy, 2, 4)):
                 copy(
-                    out=grp[:, j0:j1, :, :].rearrange("p t m j -> p m j t"),
-                    in_=d_raw[g][:].rearrange("p j (m t) -> p m j t", t=4)[:, :, :, j0:j1],
+                    out=grp[:, i0:i1, :, :].rearrange("p i m j -> p m j i"),
+                    in_=d_raw[g][:].rearrange("p j (m i) -> p m j i", i=PACK)[:, :, :, i0:i1],
                 )
-            for j0, j1 in ((0, 2), (2, 4)):
+            for i0, i1 in ((0, 2), (2, 4)):
                 nc.vector.quantize_mx(
-                    out=d_codes[g][:, P * j0 : P * j1].bitcast(E4M3),
-                    scales=d_scale[g][:, P * j0 : P * j1],
-                    in_=grp[:, j0:j1, :, :].rearrange("p t m j -> p (t m j)"),
+                    out=d_codes[g][:, P * i0 : P * i1].bitcast(E4M3),
+                    scales=d_scale[g][:, P * i0 : P * i1],
+                    in_=grp[:, i0:i1, :, :].rearrange("p i m j -> p (i m j)"),
                 )
 
-        def h_pass(g, j, q):
-            nc.tensor.matmul_mx(
-                out=h_acc[q][:, j, :],
-                lhsT=d_codes[g][:, P * j : P * (j + 1)].bitcast(E4M3),
-                lhsT_scale=d_scale[g][:, P * j : P * (j + 1)],
-                rhs=x_codes[g][:, P * q : P * (q + 1)].bitcast(E4M3),
-                rhs_scale=x_scale[g][:, P * q : P * (q + 1)],
-                start=(g == 0 and j == 0),
-                stop=(g == LAST and j == PACK - 1),
-            )
+        def h_passes(g, quarters):
+            for q in quarters:
+                for i in range(PACK):
+                    nc.tensor.matmul_mx(
+                        out=h_acc[q][:, i, :],
+                        lhsT=d_codes[g][:, P * i : P * (i + 1)].bitcast(E4M3),
+                        lhsT_scale=d_scale[g][:, P * i : P * (i + 1)],
+                        rhs=x_codes[g][:, P * q : P * (q + 1)].bitcast(E4M3),
+                        rhs_scale=x_scale[g][:, P * q : P * (q + 1)],
+                        start=(g == d_order[0] and i == 0),
+                        stop=(g == LAST and i == PACK - 1),
+                    )
 
         def w4_pass(n, g):
+            half, m = divmod(n, BANKS)
             nc.tensor.matmul_mx(
                 out=y_acc[n][:],
-                lhsT=w4[n // BANKS][:, g - NO, 2 * P * (n % BANKS) : 2 * P * (n % BANKS + 1)].bitcast(E2M1),
-                lhsT_scale=w4s[:, g - NO, P * n : P * (n + 1)],
-                rhs=x_codes[g][:].bitcast(E4M3), rhs_scale=x_scale[g][:],
-                start=(g == NO), stop=(g == NK - 1 and n < BANKS),
+                lhsT=w4[half][:, g - NO, 2 * P * m : 2 * P * (m + 1)].bitcast(E2M1),
+                lhsT_scale=w4s[half][:, g - NO, P * m : P * (m + 1)],
+                rhs=x_codes[g][:].bitcast(E4M3),
+                rhs_scale=x_scale[g][:],
+                start=(g == NO),
+                stop=(g == NK - 1 and n < LATE),
             )
 
         def w8_pass(n, g):
+            plane, m = (w8s[0], n) if n < LATE else (w8s[1 + g], n - LATE)
             nc.tensor.matmul_mx(
                 out=y_acc[n][:],
                 lhsT=w8_cols(n, n + 1)[:, g, :].bitcast(E4M3),
-                lhsT_scale=w8s[0 if n < BANKS else 1 + g][4 + 4 * g : P, P * (n % BANKS) : P * (n % BANKS + 1)],
-                rhs=x_codes[g][:].bitcast(E4M3), rhs_scale=x_scale[g][:],
-                start=(n < NT - HELD and g == (0 if n < BANKS else LAST)),
-                stop=(g == 0 and BANKS <= n < NT - HELD),
+                lhsT_scale=plane[4 + 4 * g : P, P * m : P * (m + 1)],
+                rhs=x_codes[g][:].bitcast(E4M3),
+                rhs_scale=x_scale[g][:],
+                start=(n < FIRST_HELD and g == (0 if n < LATE else LAST)),
+                stop=(g == 0 and LATE <= n < FIRST_HELD),
             )
 
         def up_pass(n):
             nc.tensor.matmul_mx(
                 out=y_acc[n][:],
-                lhsT=up[:, 2 * P * n : 2 * P * (n + 1)].bitcast(E2M1), lhsT_scale=ups[:, P * n : P * (n + 1)],
-                rhs=h_codes[:].bitcast(E4M3), rhs_scale=h_scale[:],
-                start=False, stop=True,
+                lhsT=up[:, 2 * P * n : 2 * P * (n + 1)].bitcast(E2M1),
+                lhsT_scale=ups[:, P * n : P * (n + 1)],
+                rhs=h_codes[:].bitcast(E4M3),
+                rhs_scale=h_scale[:],
+                start=False,
+                stop=True,
             )
 
-        def add_bias(n, on_scalar):
+        def copy_out_with_bias(n, on_scalar):
             if on_scalar:
                 nc.scalar.activation(out=res[n][:], in_=y_acc[n][:], func=IDENT, bias=b_col[:, n : n + 1])
             else:
@@ -221,92 +228,81 @@ def tile_mix_three_fm_bias_kernel(
 
         b_turn = psum.tile([P, P], F32, name=f"bank{BANKS - 1}")
         nc.tensor.transpose(b_turn[:], b_rows[:], ident[:])
+        quant_x(NO, x_raw[NO], X_VECTOR, 0)
         nc.scalar.activation(out=b_col[:], in_=b_turn[:, 0:NT], func=IDENT)
 
         for n in range(BANKS):
             open_bank(n, n)
         for g in range(NO, NK):
-            quant_x(g, spread_x(x_raw[g], XV))
+            if g > NO:
+                quant_x(g, x_raw[g], X_VECTOR, 0)
             for n in range(BANKS):
                 w4_pass(n, g)
-        for n in range(HELD):
-            add_bias(n, n % 2 == 0)
-        grp = spread_x(x_raw[0], XV)
-        for n in range(HELD, BANKS - 1):
-            add_bias(n, n % 2 == 0)
-        quant_x(0, grp)
-        add_bias(BANKS - 1, False)
+        for n in range(LATE):
+            copy_out_with_bias(n, n % 2 == 0)
+        quant_x(0, x_raw[0], X_VECTOR, 0)
 
-        def early_tile(n):
+        def w4_passes(n):
             open_bank(n, n % HELD)
             for g in range(NO, NK):
                 w4_pass(n, g)
 
-        def h_passes(g, quarters):
-            for q in quarters:
-                for j in range(PACK):
-                    h_pass(g, j, q)
-
-        for n in range(BANKS, NT - HELD):
-            early_tile(n)
+        for n in range(BANKS, FIRST_HELD):
+            w4_passes(n)
         quant_d(d_order[0])
-        for n in range(BANKS, NT - HELD):
+        for n in list(range(BANKS, FIRST_HELD)) + list(range(LATE, BANKS)):
             w8_pass(n, 0)
-            add_bias(n, True)
+            copy_out_with_bias(n, n % 2 == 0)
         quant_d(d_order[1])
         h_banks = range(HELD, BANKS)
         h_acc = [psum.tile([P, PACK, P], F32, name=f"bank{bank}") for bank in h_banks]
-        for i, g in enumerate(d_order[:-1]):
-            h_passes(g, range(PACK))
-            early_tile(NT - HELD + i)
-            if i + 2 < NK:
-                quant_d(d_order[i + 2])
-        for n in range(NT - HELD, NT):
+        held = list(range(FIRST_HELD, NT))
+        w4_passes(held[0])
+        for step, g in enumerate(d_order[:-1]):
+            if step + 1 < HELD:
+                w4_passes(held[step + 1])
+            h_passes(g, range(QUARTERS))
+            if step + 2 < NK:
+                quant_d(d_order[step + 2])
+        for n in held:
             w8_pass(n, 0)
 
-        def spread_h(copy, q):
-            copy(out=h_grp[:, P * q : P * (q + 1), :], in_=h_acc[q][:].rearrange("p j t -> p t j"))
-
-        def quant_h(q):
-            t0, t1 = P * q, P * (q + 1)
-            nc.vector.quantize_mx(
-                out=h_codes[:, t0:t1].bitcast(E4M3),
-                scales=h_scale[:, t0:t1],
-                in_=h_grp[:, t0:t1, :].rearrange("p t j -> p (t j)"),
-            )
-
         for half in range(2):
-            quant_x(LAST, spread_x(x_last[half], XV_LAST), half * T // 2, (half + 1) * T // 2)
+            quant_x(LAST, x_last[half], X_VECTOR_HALF, half * T // 2)
             h_passes(LAST, (2 * half, 2 * half + 1))
-        for q in (0, 2):
-            spread_h(nc.scalar.copy, q)
-            spread_h(nc.vector.tensor_copy, q + 1)
-            quant_h(q)
-            quant_h(q + 1)
+        for pair in ((0, 1), (2, 3)):
+            for copy, q in zip((nc.scalar.copy, nc.vector.tensor_copy), pair):
+                copy(out=h_grp[:, P * q : P * (q + 1), :], in_=h_acc[q][:].rearrange("p i t -> p t i"))
+            for q in pair:
+                nc.vector.quantize_mx(
+                    out=h_codes[:, P * q : P * (q + 1)].bitcast(E4M3),
+                    scales=h_scale[:, P * q : P * (q + 1)],
+                    in_=h_grp[:, P * q : P * (q + 1), :].rearrange("p t i -> p (t i)"),
+                )
 
         free = list(h_banks)
 
-        def late_passes(n):
-            if n < NT - HELD:
+        def late_w8_passes(n):
+            if n not in held:
                 open_bank(n, free[0])
                 free.remove(free[0])
-            for g in range(0 if n < BANKS else LAST, NO):
+            for g in range(0 if n < LATE else LAST, NO):
                 w8_pass(n, g)
 
-        held = list(range(NT - HELD, NT))
-        ahead = held + list(range(BANKS, BANKS + GAP_PARKED))
+        ahead = held + list(range(BANKS, BANKS + FILL))
         for n in ahead:
-            late_passes(n)
-        order = [n for pair in zip(held, range(BANKS, NT - HELD)) for n in pair] + list(range(BANKS))
+            late_w8_passes(n)
+        order = [n for pair in zip(held, range(BANKS, FIRST_HELD)) for n in pair]
+        order = order + list(range(LATE, BANKS)) + list(range(LATE))
         for n in order:
             if n not in ahead:
-                late_passes(n)
+                late_w8_passes(n)
             up_pass(n)
-            halves = 2 if n == order[-1] else 1
-            for half in range(halves):
-                cols = slice(half * T // halves, (half + 1) * T // halves)
+            pieces = 2 if n == order[-1] else 1
+            for piece in range(pieces):
+                cols = slice(piece * T // pieces, (piece + 1) * T // pieces)
                 if n in held:
-                    add_bias(n, True)
+                    copy_out_with_bias(n, True)
                 else:
                     nc.vector.tensor_add(res[n][:, cols], y_acc[n][:, cols], res[n][:, cols])
                 nc.sync.dma_start(out=out[P * n : P * (n + 1), cols], in_=res[n][:, cols])

@@ -29,8 +29,8 @@ LAST = NO - 1
 LATE = HELD
 W8_PARTS = ((0, LATE), (LATE, NT))
 FILL = 2
-X_VECTOR = 320
-X_VECTOR_HALF = 160
+LAST_PIECES = ((0, 2), (2, 3), (3, 4))
+X_VECTOR = 80
 
 
 def tile_mix_three_fm_bias_kernel(
@@ -44,7 +44,7 @@ def tile_mix_three_fm_bias_kernel(
         ctx.enter_context(tc.manual_schedule())
 
         x_raw = {g: keep.tile([P, PACK, T], F32, name=f"x_raw{g}") for g in range(NK) if g != LAST}
-        x_last = [keep.tile([P, PACK, T // 2], F32, name=f"x_last{half}") for half in range(2)]
+        x_last = [keep.tile([P, PACK, P * (q1 - q0)], F32, name=f"x_last{q0}") for q0, q1 in LAST_PIECES]
         d_raw = [keep.tile([P, PACK, R], F32, name=f"d_raw{g}") for g in range(NK)]
         x_codes = [keep.tile([P, T], U32, name=f"x_codes{g}", align_bytes=64) for g in range(NK)]
         x_scale = [keep.tile([P, T], U8, name=f"x_scale{g}", align_bytes=64) for g in range(NK)]
@@ -128,8 +128,8 @@ def tile_mix_three_fm_bias_kernel(
             load_pass(d_raw[g], down, g)
         load_w8(FIRST_HELD, NT, 0, 1)
         x_rows = x[KP * LAST : KP * (LAST + 1), :].rearrange("(p j) t -> p j t", j=PACK)
-        for half in range(2):
-            nc.sync.dma_start(out=x_last[half][:], in_=x_rows[:, :, half * T // 2 : (half + 1) * T // 2])
+        for raw, (q0, q1) in zip(x_last, LAST_PIECES):
+            nc.sync.dma_start(out=raw[:], in_=x_rows[:, :, P * q0 : P * q1])
         load_w8(BANKS, NT, LAST, NO)
         for r in range(4):
             nc.sync.dma_start(out=ups[r:P:32, :].bitcast(I32), in_=up_scales[0, r:16:4, :].bitcast(I32))
@@ -137,8 +137,9 @@ def tile_mix_three_fm_bias_kernel(
         load_w8(LATE, BANKS, LAST, NO)
         load_w8(0, LATE, 0, NO)
 
-        def quant_x(g, raw, on_vector, t0):
+        def quant_x(g, raw, t0):
             width = raw.shape[2]
+            on_vector = X_VECTOR * width // P
             grp = group.tile([P, width, PACK], BF16, name="x_grp", align_bytes=64)
             for copy, c0, c1 in ((nc.vector.tensor_copy, 0, on_vector), (nc.scalar.copy, on_vector, width)):
                 copy(
@@ -228,19 +229,19 @@ def tile_mix_three_fm_bias_kernel(
 
         b_turn = psum.tile([P, P], F32, name=f"bank{BANKS - 1}")
         nc.tensor.transpose(b_turn[:], b_rows[:], ident[:])
-        quant_x(NO, x_raw[NO], X_VECTOR, 0)
+        quant_x(NO, x_raw[NO], 0)
         nc.scalar.activation(out=b_col[:], in_=b_turn[:, 0:NT], func=IDENT)
 
         for n in range(BANKS):
             open_bank(n, n)
         for g in range(NO, NK):
             if g > NO:
-                quant_x(g, x_raw[g], X_VECTOR, 0)
+                quant_x(g, x_raw[g], 0)
             for n in range(BANKS):
                 w4_pass(n, g)
         for n in range(LATE):
             copy_out_with_bias(n, n % 2 == 0)
-        quant_x(0, x_raw[0], X_VECTOR, 0)
+        quant_x(0, x_raw[0], 0)
 
         def w4_passes(n):
             open_bank(n, n % HELD)
@@ -267,18 +268,26 @@ def tile_mix_three_fm_bias_kernel(
         for n in held:
             w8_pass(n, 0)
 
-        for half in range(2):
-            quant_x(LAST, x_last[half], X_VECTOR_HALF, half * T // 2)
-            h_passes(LAST, (2 * half, 2 * half + 1))
-        for pair in ((0, 1), (2, 3)):
-            for copy, q in zip((nc.scalar.copy, nc.vector.tensor_copy), pair):
-                copy(out=h_grp[:, P * q : P * (q + 1), :], in_=h_acc[q][:].rearrange("p i t -> p t i"))
-            for q in pair:
-                nc.vector.quantize_mx(
-                    out=h_codes[:, P * q : P * (q + 1)].bitcast(E4M3),
-                    scales=h_scale[:, P * q : P * (q + 1)],
-                    in_=h_grp[:, P * q : P * (q + 1), :].rearrange("p t i -> p (t i)"),
-                )
+        for raw, (q0, q1) in zip(x_last, LAST_PIECES):
+            quant_x(LAST, raw, P * q0)
+            h_passes(LAST, range(q0, q1))
+
+        def copy_h(copy, q):
+            copy(out=h_grp[:, P * q : P * (q + 1), :], in_=h_acc[q][:].rearrange("p i t -> p t i"))
+
+        def quant_h(q):
+            nc.vector.quantize_mx(
+                out=h_codes[:, P * q : P * (q + 1)].bitcast(E4M3),
+                scales=h_scale[:, P * q : P * (q + 1)],
+                in_=h_grp[:, P * q : P * (q + 1), :].rearrange("p t i -> p (t i)"),
+            )
+
+        for q in range(QUARTERS - 1):
+            copy_h(nc.scalar.copy, q)
+        quant_h(0)
+        copy_h(nc.vector.tensor_copy, QUARTERS - 1)
+        for q in range(1, QUARTERS):
+            quant_h(q)
 
         free = list(h_banks)
 
@@ -298,12 +307,9 @@ def tile_mix_three_fm_bias_kernel(
             if n not in ahead:
                 late_w8_passes(n)
             up_pass(n)
-            pieces = 2 if n == order[-1] else 1
-            for piece in range(pieces):
-                cols = slice(piece * T // pieces, (piece + 1) * T // pieces)
-                if n in held:
-                    copy_out_with_bias(n, True)
-                else:
-                    nc.vector.tensor_add(res[n][:, cols], y_acc[n][:, cols], res[n][:, cols])
-                nc.sync.dma_start(out=out[P * n : P * (n + 1), cols], in_=res[n][:, cols])
+            if n in held:
+                copy_out_with_bias(n, True)
+            else:
+                nc.vector.tensor_add(res[n][:], y_acc[n][:], res[n][:])
+            nc.sync.dma_start(out=out[P * n : P * (n + 1), :], in_=res[n][:])
             free.append(bank_of[n])

from contextlib import ExitStack

import concourse.mybir as mybir
from concourse.masks import make_identity

O, K, R, M, T = 1024, 2560, 512, 2048, 512
FLOPS = 2 * K * R * T + 2 * (K + R) * M * T

F32 = mybir.dt.float32
BF16 = mybir.dt.bfloat16
I32 = mybir.dt.int32
U32 = mybir.dt.uint32
U8 = mybir.dt.uint8
E4M3 = mybir.dt.float8_e4m3fn_x4
E2M1 = mybir.dt.float4_e2m1fn_x4
IDENT = mybir.ActivationFunctionType.Identity

P = 128
PACK = 4
KP = P * PACK
NK = K // KP
NO = O // KP
NT = M // P
BANKS = 8
QUARTERS = T // P
HELD = BANKS - QUARTERS
FIRST_HELD = NT - HELD
LAST = NO - 1
LATE = HELD
W8_PARTS = ((0, LATE), (LATE, NT))
FILL = 2
LAST_PIECES = ((0, 2), (2, 3), (3, 4))
X_VECTOR = 80


def tile_mix_three_fm_bias_kernel(
    tc, x, w8_words, w8_scales, w4_words, w4_scales, down, up_words, up_scales, b, out
):
    nc = tc.nc
    with ExitStack() as ctx:
        keep = ctx.enter_context(tc.tile_pool(name="keep", bufs=1))
        group = ctx.enter_context(tc.tile_pool(name="group", bufs=2))
        psum = ctx.enter_context(tc.psum_pool(name="psum", bufs=1))
        ctx.enter_context(tc.manual_schedule())

        x_raw = {g: keep.tile([P, PACK, T], F32, name=f"x_raw{g}") for g in range(NK) if g != LAST}
        x_last = [keep.tile([P, PACK, P * (q1 - q0)], F32, name=f"x_last{q0}") for q0, q1 in LAST_PIECES]
        d_raw = [keep.tile([P, PACK, R], F32, name=f"d_raw{g}") for g in range(NK)]
        x_codes = [keep.tile([P, T], U32, name=f"x_codes{g}", align_bytes=64) for g in range(NK)]
        x_scale = [keep.tile([P, T], U8, name=f"x_scale{g}", align_bytes=64) for g in range(NK)]
        d_codes = [keep.tile([P, R], U32, name=f"d_codes{g}", align_bytes=64) for g in range(NK)]
        d_scale = [keep.tile([P, R], U8, name=f"d_scale{g}", align_bytes=64) for g in range(NK)]
        w8 = [keep.tile([P, NO, P * (n1 - n0)], U32, name=f"w8_{n0}", align_bytes=64) for n0, n1 in W8_PARTS]
        w4 = [keep.tile([P, NK - NO, M], U8, name=f"w4_{half}", align_bytes=64) for half in range(2)]
        w8s = [
            keep.tile([P, width], U8, name=f"w8s_{i}", align_bytes=64)
            for i, width in enumerate((P * LATE, M - P * LATE, M - P * LATE))
        ]
        w4s = [keep.tile([P, NK - NO, M // 2], U8, name=f"w4s_{half}", align_bytes=64) for half in range(2)]
        up = keep.tile([P, 2 * M], U8, name="up", align_bytes=64)
        ups = keep.tile([P, M], U8, name="ups", align_bytes=64)
        b_rows = keep.tile([P, P], F32, name="b_rows")
        ident = keep.tile([P, P], F32, name="ident")
        b_col = keep.tile([P, NT], F32, name="b_col")
        h_grp = keep.tile([P, T, PACK], BF16, name="h_grp", align_bytes=64)
        h_codes = keep.tile([P, T], U32, name="h_codes", align_bytes=64)
        h_scale = keep.tile([P, T], U8, name="h_scale", align_bytes=64)
        res = [keep.tile([P, T], F32, name=f"res{n}") for n in range(NT)]

        nc.gpsimd.memset(b_rows[:], 0.0)
        nc.vector.memset(w4s[0][:].rearrange("p a n -> p (a n)").bitcast(I32), 0)
        for plane in w8s:
            nc.vector.memset(plane[:].bitcast(I32), 0)
        nc.vector.memset(w4s[1][:].rearrange("p a n -> p (a n)").bitcast(I32), 0)
        nc.vector.memset(ups[:].bitcast(I32), 0)
        make_identity(nc, ident[:])

        w8_view = w8_words.rearrange("a p n i -> p a (n i)")

        def load_pass(raw, source, g):
            nc.sync.dma_start(
                out=raw[:].rearrange("p j c -> p (j c)"),
                in_=source[KP * g : KP * (g + 1), :].rearrange("(p j) c -> p (j c)", j=PACK),
            )

        def w8_cols(n0, n1):
            part = 0 if n0 < LATE else 1
            first = W8_PARTS[part][0]
            return w8[part][:, :, P * (n0 - first) : P * (n1 - first)]

        def load_w8(n0, n1, g0, g1):
            nc.sync.dma_start(
                out=w8_cols(n0, n1)[:, g0:g1, :].bitcast(I32),
                in_=w8_view[:, g0:g1, PACK * P * n0 : PACK * P * n1].bitcast(I32),
            )

        def load_w4s(half):
            rows = w4_scales.rearrange("a q n -> q a n")[:, :, half * M // 2 : (half + 1) * M // 2]
            for r in range(4):
                nc.sync.dma_start(out=w4s[half][r:P:32].bitcast(I32), in_=rows[r:16:4].bitcast(I32))

        def load_w8s(queue, g):
            for r in range(4):
                queue.dma_start(
                    out=w8s[1 + g][4 + 4 * g + r : P : 32, :].bitcast(I32),
                    in_=w8_scales[g, r:16:4, P * LATE : M].bitcast(I32),
                )

        for g in range(NO, NK):
            load_pass(x_raw[g], x, g)
            if g == NO:
                nc.sync.dma_start(out=b_rows[0:NT, :], in_=b.rearrange("(n p) -> n p", p=P))
                load_w4s(0)
                load_w8s(nc.gpsimd, LAST)
                for quad in range(4):
                    nc.gpsimd.dma_start(
                        out=w8s[0][32 * quad + 4 : 32 * quad + 12, :].bitcast(I32),
                        in_=w8_scales[:, 4 * quad : 4 * quad + 4, 0 : P * LATE].bitcast(I32),
                    )
            nc.sync.dma_start(out=w4[0][:, g - NO, :].bitcast(I32), in_=w4_words[g - NO, :, 0:M].bitcast(I32))
        load_w4s(1)
        nc.sync.dma_start(out=w4[1][:].bitcast(I32), in_=w4_words.rearrange("a p n -> p a n")[:, :, M:].bitcast(I32))
        load_pass(x_raw[0], x, 0)
        load_w8s(nc.sync, 0)
        load_w8(LATE, FIRST_HELD, 0, 1)
        d_order = [g for g in range(NK) if g != LAST] + [LAST]
        for g in d_order:
            load_pass(d_raw[g], down, g)
        load_w8(FIRST_HELD, NT, 0, 1)
        x_rows = x[KP * LAST : KP * (LAST + 1), :].rearrange("(p j) t -> p j t", j=PACK)
        for raw, (q0, q1) in zip(x_last, LAST_PIECES):
            nc.sync.dma_start(out=raw[:], in_=x_rows[:, :, P * q0 : P * q1])
        load_w8(BANKS, NT, LAST, NO)
        for r in range(4):
            nc.sync.dma_start(out=ups[r:P:32, :].bitcast(I32), in_=up_scales[0, r:16:4, :].bitcast(I32))
        nc.sync.dma_start(out=up[:].bitcast(I32), in_=up_words[0].bitcast(I32))
        load_w8(LATE, BANKS, LAST, NO)
        load_w8(0, LATE, 0, NO)

        def quant_x(g, raw, t0):
            width = raw.shape[2]
            on_vector = X_VECTOR * width // P
            grp = group.tile([P, width, PACK], BF16, name="x_grp", align_bytes=64)
            for copy, c0, c1 in ((nc.vector.tensor_copy, 0, on_vector), (nc.scalar.copy, on_vector, width)):
                copy(
                    out=grp[:, c0:c1, :].rearrange("p (c i) j -> p c j i", i=4),
                    in_=raw[:, :, c0:c1].rearrange("p j (c i) -> p c j i", i=4),
                )
            nc.vector.quantize_mx(
                out=x_codes[g][:, t0 : t0 + width].bitcast(E4M3),
                scales=x_scale[g][:, t0 : t0 + width],
                in_=grp[:].rearrange("p t j -> p (t j)"),
            )

        def quant_d(g):
            grp = group.tile([P, PACK, P, PACK], BF16, name="d_grp", align_bytes=64)
            for copy, i0, i1 in ((nc.vector.tensor_copy, 0, 2), (nc.scalar.copy, 2, 4)):
                copy(
                    out=grp[:, i0:i1, :, :].rearrange("p i m j -> p m j i"),
                    in_=d_raw[g][:].rearrange("p j (m i) -> p m j i", i=PACK)[:, :, :, i0:i1],
                )
            for i0, i1 in ((0, 2), (2, 4)):
                nc.vector.quantize_mx(
                    out=d_codes[g][:, P * i0 : P * i1].bitcast(E4M3),
                    scales=d_scale[g][:, P * i0 : P * i1],
                    in_=grp[:, i0:i1, :, :].rearrange("p i m j -> p (i m j)"),
                )

        def h_passes(g, quarters):
            for q in quarters:
                for i in range(PACK):
                    nc.tensor.matmul_mx(
                        out=h_acc[q][:, i, :],
                        lhsT=d_codes[g][:, P * i : P * (i + 1)].bitcast(E4M3),
                        lhsT_scale=d_scale[g][:, P * i : P * (i + 1)],
                        rhs=x_codes[g][:, P * q : P * (q + 1)].bitcast(E4M3),
                        rhs_scale=x_scale[g][:, P * q : P * (q + 1)],
                        start=(g == d_order[0] and i == 0),
                        stop=(g == LAST and i == PACK - 1),
                    )

        def w4_pass(n, g):
            half, m = divmod(n, BANKS)
            nc.tensor.matmul_mx(
                out=y_acc[n][:],
                lhsT=w4[half][:, g - NO, 2 * P * m : 2 * P * (m + 1)].bitcast(E2M1),
                lhsT_scale=w4s[half][:, g - NO, P * m : P * (m + 1)],
                rhs=x_codes[g][:].bitcast(E4M3),
                rhs_scale=x_scale[g][:],
                start=(g == NO),
                stop=(g == NK - 1 and n < LATE),
            )

        def w8_pass(n, g):
            plane, m = (w8s[0], n) if n < LATE else (w8s[1 + g], n - LATE)
            nc.tensor.matmul_mx(
                out=y_acc[n][:],
                lhsT=w8_cols(n, n + 1)[:, g, :].bitcast(E4M3),
                lhsT_scale=plane[4 + 4 * g : P, P * m : P * (m + 1)],
                rhs=x_codes[g][:].bitcast(E4M3),
                rhs_scale=x_scale[g][:],
                start=(n < FIRST_HELD and g == (0 if n < LATE else LAST)),
                stop=(g == 0 and LATE <= n < FIRST_HELD),
            )

        def up_pass(n):
            nc.tensor.matmul_mx(
                out=y_acc[n][:],
                lhsT=up[:, 2 * P * n : 2 * P * (n + 1)].bitcast(E2M1),
                lhsT_scale=ups[:, P * n : P * (n + 1)],
                rhs=h_codes[:].bitcast(E4M3),
                rhs_scale=h_scale[:],
                start=False,
                stop=True,
            )

        def copy_out_with_bias(n, on_scalar):
            if on_scalar:
                nc.scalar.activation(out=res[n][:], in_=y_acc[n][:], func=IDENT, bias=b_col[:, n : n + 1])
            else:
                nc.vector.tensor_scalar_add(res[n][:], y_acc[n][:], b_col[:, n : n + 1])

        y_acc = {}
        bank_of = {}

        def open_bank(n, bank):
            bank_of[n] = bank
            y_acc[n] = psum.tile([P, T], F32, name=f"bank{bank}")

        b_turn = psum.tile([P, P], F32, name=f"bank{BANKS - 1}")
        nc.tensor.transpose(b_turn[:], b_rows[:], ident[:])
        quant_x(NO, x_raw[NO], 0)
        nc.scalar.activation(out=b_col[:], in_=b_turn[:, 0:NT], func=IDENT)

        for n in range(BANKS):
            open_bank(n, n)
        for g in range(NO, NK):
            if g > NO:
                quant_x(g, x_raw[g], 0)
            for n in range(BANKS):
                w4_pass(n, g)
        for n in range(LATE):
            copy_out_with_bias(n, n % 2 == 0)
        quant_x(0, x_raw[0], 0)

        def w4_passes(n):
            open_bank(n, n % HELD)
            for g in range(NO, NK):
                w4_pass(n, g)

        for n in range(BANKS, FIRST_HELD):
            w4_passes(n)
        quant_d(d_order[0])
        for n in list(range(BANKS, FIRST_HELD)) + list(range(LATE, BANKS)):
            w8_pass(n, 0)
            copy_out_with_bias(n, n % 2 == 0)
        quant_d(d_order[1])
        h_banks = range(HELD, BANKS)
        h_acc = [psum.tile([P, PACK, P], F32, name=f"bank{bank}") for bank in h_banks]
        held = list(range(FIRST_HELD, NT))
        w4_passes(held[0])
        for step, g in enumerate(d_order[:-1]):
            if step + 1 < HELD:
                w4_passes(held[step + 1])
            h_passes(g, range(QUARTERS))
            if step + 2 < NK:
                quant_d(d_order[step + 2])
        for n in held:
            w8_pass(n, 0)

        for raw, (q0, q1) in zip(x_last, LAST_PIECES):
            quant_x(LAST, raw, P * q0)
            h_passes(LAST, range(q0, q1))

        def copy_h(copy, q):
            copy(out=h_grp[:, P * q : P * (q + 1), :], in_=h_acc[q][:].rearrange("p i t -> p t i"))

        def quant_h(q):
            nc.vector.quantize_mx(
                out=h_codes[:, P * q : P * (q + 1)].bitcast(E4M3),
                scales=h_scale[:, P * q : P * (q + 1)],
                in_=h_grp[:, P * q : P * (q + 1), :].rearrange("p t i -> p (t i)"),
            )

        for q in range(QUARTERS - 1):
            copy_h(nc.scalar.copy, q)
        quant_h(0)
        copy_h(nc.vector.tensor_copy, QUARTERS - 1)
        for q in range(1, QUARTERS):
            quant_h(q)

        free = list(h_banks)

        def late_w8_passes(n):
            if n not in held:
                open_bank(n, free[0])
                free.remove(free[0])
            for g in range(0 if n < LATE else LAST, NO):
                w8_pass(n, g)

        ahead = held + list(range(BANKS, BANKS + FILL))
        for n in ahead:
            late_w8_passes(n)
        order = [n for pair in zip(held, range(BANKS, FIRST_HELD)) for n in pair]
        order = order + list(range(LATE, BANKS)) + list(range(LATE))
        for n in order:
            if n not in ahead:
                late_w8_passes(n)
            up_pass(n)
            if n in held:
                copy_out_with_bias(n, True)
            else:
                nc.vector.tensor_add(res[n][:], y_acc[n][:], res[n][:])
            nc.sync.dma_start(out=out[P * n : P * (n + 1), :], in_=res[n][:])
            free.append(bank_of[n])
